import numpy as np
import ml_dtypes


def mxq(x, axis, fmt="e4m3"):
    dtype, down = {"e4m3": (ml_dtypes.float8_e4m3fn, 7), "e5m2": (ml_dtypes.float8_e5m2, 14)}[fmt]
    v = np.moveaxis(np.asarray(x, np.float32).astype(ml_dtypes.bfloat16).astype(np.float64), axis, -1)
    blocks = v.reshape(v.shape[:-1] + (-1, 32))
    amax = np.abs(blocks).max(-1, keepdims=True)
    byte = np.maximum(np.where(amax > 0, np.frexp(amax)[1] - 1 + 127, 0) - down, 1)
    scale = np.exp2(byte - 127.0)
    codes = (blocks / scale).astype(np.float32).astype(dtype).astype(np.float64)
    return np.moveaxis((codes * scale).reshape(v.shape), -1, axis)


WIDE = False


def mx_kscale(k):
    if not WIDE:
        return np.ones(k)
    levels = np.array([10, -10, 5, -5, 0])
    if k % 512:
        return np.exp2(np.random.permutation(np.resize(levels, k // 32))).repeat(32)
    a = np.empty((k // 512, 16))
    for p in range(k // 512):
        a[p, :8] = np.random.permutation(np.resize(levels, 8))
        for g in range(8):
            far = levels[np.abs(levels - a[p, g]) >= 10]
            a[p, g + 8] = far[np.random.randint(len(far))]
    return np.exp2(a.ravel()).repeat(32)


BF16 = ml_dtypes.bfloat16


def bf(x):
    return np.asarray(x, np.float32).astype(BF16)


def f64(x):
    return np.asarray(x).astype(np.float64)

def planes(Y):
    n, m = Y.shape
    b = f64(bf(Y)).reshape(n // 32, 32, m)
    amax = np.abs(b).max(1)
    byte = np.clip(np.where(amax > 0, np.frexp(amax)[1] - 1 + 127 - 7, 1), 1, 254)
    codes = (b * np.exp2(127.0 - byte)[:, None, :]).reshape(n, m).astype(np.float32).astype(ml_dtypes.float8_e4m3fn).view(np.uint8)
    words = codes.reshape(n // 512, 128, 4, m).transpose(0, 1, 3, 2)
    return np.ascontiguousarray(words), np.ascontiguousarray(byte.astype(np.uint8).reshape(n // 512, 16, m))


M, F, C, D = 1280, 3072, 512, 1024

def setup_inputs():
    noise = np.random.randn
    t = mx_kscale(F)
    s = mx_kscale(C)
    spread = np.exp(0.7 * noise(D))
    return {
        "pre": bf(noise(M, F)),
        "b_enc": bf(-0.25 + 0.3 * noise(F)),
        "g": bf(t * np.exp(0.3 * noise(F))),
        "w_dec": bf(1.5 / np.sqrt(F) * noise(F, D) * spread / t[:, None]),
        "b_dec": bf(0.3 * noise(D) * spread),
        "r": bf(np.exp(0.3 * noise(M, 1))),
        "x": bf(noise(M, C) * s),
        "w_skip": bf(0.7 / np.sqrt(C) * noise(C, D) * spread / s[:, None]),
    }

def reference(pre, b_enc, g, w_dec, b_dec, r, x, w_skip):
    z = np.maximum(f64(pre) + f64(b_enc), 0.0) * f64(g)
    dec = mxq(z, 1, "e4m3") @ mxq(f64(w_dec), 0, "e4m3")
    skip = mxq(f64(x), 1, "e4m3") @ mxq(f64(w_skip), 0, "e4m3")
    y = (dec + f64(b_dec)) * f64(r) + skip
    Y = y.T
    words, scales = planes(Y)
    return y, words, scales

@@ -1,0 +1,702 @@
+from contextlib import ExitStack
+
+import concourse.mybir as mybir
+from concourse.masks import make_identity
+
+M, F, C, D = 1280, 3072, 512, 1024
+FLOPS = 2 * M * (F + C) * D
+
+F32 = mybir.dt.float32
+BF16 = mybir.dt.bfloat16
+U32 = mybir.dt.uint32
+I32 = mybir.dt.int32
+U8 = mybir.dt.uint8
+FP8X4 = mybir.dt.float8_e4m3fn_x4
+ALU = mybir.AluOpType
+ACT = mybir.ActivationFunctionType
+
+P = 128
+PACK = 4
+KP = P * PACK
+G = F // KP
+HALF = 512
+CHUNKS = [(0, 4), (4, 4), (8, 2)]
+B_ROW, R_ROW = 8, 16
+
+
+def tile_sae_relu_decode_skip_g1_kernel(tc, pre, b_enc, g, w_dec, b_dec, r, x, w_skip, out_0, out_1, out_2):
+    nc = tc.nc
+    with ExitStack() as ctx:
+        keep = ctx.enter_context(tc.tile_pool(name="keep", bufs=1))
+        work = ctx.enter_context(tc.tile_pool(name="work", bufs=1))
+        psum = ctx.enter_context(tc.psum_pool(name="psum", bufs=1))
+        ctx.enter_context(tc.manual_schedule())
+
+        ident = keep.tile([P, P], F32, name="ident")
+        ident_bf = keep.tile([P, P], BF16, name="ident_bf")
+        vec_rows = keep.tile([P, KP], BF16, name="vec_rows")
+        sign = keep.tile([P, G, PACK], F32, name="sign")
+        g_abs = keep.tile([P, G, PACK], F32, name="g_abs")
+        gb = keep.tile([P, G, PACK], F32, name="gb")
+        r_col = keep.tile([P, M // P], F32, name="r_col")
+        b_all = keep.tile([P, D], BF16, name="b_all")
+        y_codes = [keep.tile([P, M], U32, name="y_codes%d" % n, align_bytes=64) for n in range(2)]
+        y_scales = [keep.tile([P, M], U8, name="y_scales%d" % n, align_bytes=64) for n in range(2)]
+
+        raw, slots, grouped, codes, scales, banks, part, ybf = {}, {}, {}, {}, {}, {}, {}, {}
+
+        free_banks = list(range(8))
+        held = {}
+
+        def take(key, shape, dtype):
+            held[key] = free_banks.pop(0)
+            banks[key] = psum.tile(shape, dtype, name="bank%d" % held[key])
+            return banks[key]
+
+        def release(key):
+            free_banks.append(held.pop(key))
+
+        def width(u):
+            return CHUNKS[u[1]][1] * P if u[0] in "zxy" else HALF
+
+        def constants_load():
+            nc.vector.memset(vec_rows[:], 0.0)
+            make_identity(nc, ident[:])
+            nc.scalar.dma_start(out=vec_rows[0:G, :], in_=g.rearrange("(c k) -> c k", k=KP))
+            nc.scalar.dma_start(out=vec_rows[B_ROW:B_ROW + G, :], in_=b_enc.rearrange("(c k) -> c k", k=KP))
+            nc.scalar.dma_start(out=vec_rows[R_ROW:R_ROW + M // P, 0:P], in_=r.rearrange("(m p) o -> m (p o)", p=P))
+            nc.vector.tensor_copy(out=ident_bf[:], in_=ident[:])
+
+        def constants_turn():
+            bank = take("vec", [P, 2, P], F32)
+            words = vec_rows[:].bitcast(F32)
+            for u in range(2):
+                nc.tensor.transpose(bank[:, u, :], words[:, u::2], ident[:])
+            r_bank = take("r", [P, P], BF16)
+            nc.tensor.transpose(r_bank[:], vec_rows[:, 0:P], ident_bf[:])
+            vals = bank[:].rearrange("p u c -> p (u c)").bitcast(BF16).rearrange("p (u c e) -> p c u e", u=2, e=2)
+            g_t, b_t = vals[:, 0:G], vals[:, B_ROW:B_ROW + G]
+            split = lambda t: t[:].rearrange("p c (u e) -> p c u e", e=2)
+            nc.vector.tensor_scalar(out=split(sign), in0=g_t, scalar1=0.0, scalar2=2.0, op0=ALU.is_ge, op1=ALU.mult)
+            nc.vector.tensor_scalar(out=sign[:], in0=sign[:], scalar1=-1.0, scalar2=None, op0=ALU.add)
+            nc.vector.tensor_tensor(out=split(g_abs), in0=g_t, in1=split(sign), op=ALU.mult)
+            nc.vector.tensor_tensor(out=split(gb), in0=b_t, in1=split(g_abs), op=ALU.mult)
+            nc.scalar.copy(out=r_col[:], in_=r_bank[:, R_ROW:R_ROW + M // P])
+            release("vec")
+            release("r")
+
+        def bias_load():
+            nc.sync.dma_start(out=b_all[:], in_=b_dec.partition_broadcast(P))
+
+        def load(u):
+            kind, a, b = u
+            t = work.tile([P, PACK, KP], BF16, name="raw", tag="raw", bufs=10)
+            raw[u] = t
+            if kind in "zx":
+                m0, nm = CHUNKS[a]
+                src = (pre if kind == "z" else x)[m0 * P:(m0 + nm) * P, b * KP:(b + 1) * KP]
+                nc.sync.dma_start(out=t[:, 0:nm, :], in_=src.rearrange("(m p) k -> p m k", p=P))
+            else:
+                src = (w_dec if kind == "w" else w_skip)[b * KP:(b + 1) * KP, a * HALF:(a + 1) * HALF]
+                nc.sync.dma_start(out=t[:], in_=src.rearrange("(p j) d -> p j d", j=PACK))
+
+        def turn_z(u, h):
+            nm = CHUNKS[u[1]][1]
+            bank = take((u, h), [P, nm * P], F32)
+            for m in range(nm):
+                nc.tensor.transpose(bank[:, m * P:(m + 1) * P], raw[u][:, m, :].bitcast(F32)[:, h::2], ident[:])
+
+        def encode(u, h):
+            w = width(u)
+            if u not in slots:
+                slots[u] = work.tile([P, PACK, KP], BF16, name="slots", tag="slots", bufs=3)
+            t = slots[u]
+            for j in range(2 * h, 2 * h + 2):
+                src = banks[u, j // 2][:].bitcast(BF16)[:, j % 2::2]
+                nc.scalar.activation(out=t[:, j, 0:w], in_=src, func=ACT.Relu,
+                                     bias=gb[:, u[2], j:j + 1], scale=g_abs[:, u[2], j:j + 1])
+                if j % 2:
+                    release((u, j // 2))
+
+        def sign_w(u):
+            slots[u] = raw[u]
+            for j in range(PACK):
+                nc.vector.tensor_scalar(out=raw[u][:, j, :], in0=raw[u][:, j, :], scalar1=sign[:, u[2], j:j + 1],
+                                        scalar2=None, op0=ALU.mult)
+
+        def new_grouped(u):
+            if u not in grouped:
+                grouped[u] = work.tile([P, KP * PACK], BF16, name="grouped", tag="grouped", bufs=4, align_bytes=64)
+            return grouped[u]
+
+        def interleave(u, c0, c1, on_scalar):
+            src = slots.get(u, raw[u])[:, :, c0:c1].rearrange("p t (c i) -> p c t i", i=4)
+            dst = new_grouped(u)[:, c0 * PACK:c1 * PACK].rearrange("p (c i t) -> p c t i", i=4, t=PACK)
+            if on_scalar:
+                nc.scalar.copy(out=dst, in_=src)
+            else:
+                nc.vector.tensor_copy(out=dst, in_=src)
+
+        def quantize(u):
+            w = width(u)
+            name = "%s%d%d" % u
+            codes[u] = keep.tile([P, w], U32, name="codes_" + name, align_bytes=64)
+            scales[u] = keep.tile([P, w], U8, name="scales_" + name, align_bytes=64)
+            nc.vector.quantize_mx(out=codes[u][:].bitcast(FP8X4), scales=scales[u][:], in_=grouped[u][:, 0:w * PACK])
+
+        def turn_words(u, pair, words_of):
+            bank = take((u, pair), [P, 2, 2, P], F32)
+            for m in range(2):
+                for h in range(2):
+                    nc.tensor.transpose(bank[:, m, h, :], words_of(2 * pair + m, h), ident[:])
+
+        def turn_x(u, pair):
+            turn_words(u, pair, lambda m, h: raw[u][:, m, :].bitcast(F32)[:, h::2])
+
+        def turn_y(u, pair):
+            m0 = CHUNKS[u[1]][0]
+            turn_words(u, pair, lambda m, h: ybf[m0 + m, u[2]][:].bitcast(F32)[:, h * P:(h + 1) * P])
+
+        def copy_words(u, pair, on_scalar):
+            dst = new_grouped(u)[:].bitcast(F32)[:, pair * KP:(pair + 1) * KP].rearrange("p (m c h) -> p m c h", m=2, h=2)
+            src = banks[u, pair][:].rearrange("p m h c -> p m c h")
+            if on_scalar:
+                nc.scalar.copy(out=dst, in_=src)
+            else:
+                nc.vector.tensor_copy(out=dst, in_=src)
+            release((u, pair))
+
+        def mx(out, a, m, b, start, stop):
+            cols = slice((m - CHUNKS[a[1]][0]) * P, (m - CHUNKS[a[1]][0] + 1) * P)
+            nc.tensor.matmul_mx(out=out[:], lhsT=codes[a][:, cols].bitcast(FP8X4), lhsT_scale=scales[a][:, cols],
+                                rhs=codes[b][:].bitcast(FP8X4), rhs_scale=scales[b][:], start=start, stop=stop)
+
+        def decode(c, m, n, k):
+            if k == 0:
+                take(("acc", m, n), [P, HALF], F32)
+            mx(banks["acc", m, n], ("z", c, k), m, ("w", n, k), k == 0, k == G - 1)
+
+        def skip(c, m, n):
+            mx(take(("skip", m, n), [P, HALF], F32), ("x", c, 0), m, ("s", n, 0), True, True)
+
+        def add_bias(m, n):
+            part[m, n] = work.tile([P, HALF], F32, name="y", tag="y", bufs=10)
+            nc.vector.scalar_tensor_tensor(out=part[m, n][:], in0=b_all[:, n * HALF:(n + 1) * HALF], scalar=r_col[:, m:m + 1],
+                                           in1=banks["skip", m, n][:], op0=ALU.mult, op1=ALU.add)
+            release(("skip", m, n))
+
+        def finish(m, n):
+            y = part[m, n]
+            nc.vector.scalar_tensor_tensor(out=y[:], in0=banks["acc", m, n][:], scalar=r_col[:, m:m + 1], in1=y[:],
+                                           op0=ALU.mult, op1=ALU.add)
+            release(("acc", m, n))
+
+        def store_y(m, n):
+            nc.sync.dma_start(out=out_0[m * P:(m + 1) * P, n * HALF:(n + 1) * HALF], in_=part[m, n][:])
+
+        def round_y(m, n, on_scalar):
+            ybf[m, n] = work.tile([P, HALF], BF16, name="ybf", tag="ybf", bufs=4)
+            dst = ybf[m, n][:].rearrange("p (h q e) -> p h q e", h=2, e=2)
+            src = part[m, n][:].rearrange("p (q h e) -> p h q e", h=2, e=2)
+            if on_scalar:
+                nc.scalar.copy(out=dst, in_=src)
+            else:
+                nc.vector.tensor_copy(out=dst, in_=src)
+
+        def quantize_y(u):
+            c, n = u[1], u[2]
+            cols = slice(CHUNKS[c][0] * P, CHUNKS[c][0] * P + width(u))
+            nc.vector.quantize_mx(out=y_codes[n][:, cols].bitcast(FP8X4), scales=y_scales[n][:, cols],
+                                  in_=grouped[u][:, 0:width(u) * PACK])
+
+        def store_words(u):
+            c, n = u[1], u[2]
+            cols = slice(CHUNKS[c][0] * P, CHUNKS[c][0] * P + width(u))
+            dst = out_1[n].rearrange("p m t -> p (m t)").bitcast(I32)
+            nc.sync.dma_start(out=dst[:, cols], in_=y_codes[n][:, cols].bitcast(I32))
+
+        def store_scales(n):
+            for q in range(4):
+                eng = nc.scalar if q % 2 else nc.sync
+                eng.dma_start(out=out_2[n, 4 * q:4 * q + 4, :].bitcast(I32),
+                              in_=y_scales[n][32 * q:32 * q + 4, :].bitcast(I32))
+
+        constants_load()
+        load(("w", 0, 0))
+        load(("s", 0, 0))
+        load(("z", 0, 5))
+        load(("w", 0, 1))
+        load(("z", 0, 0))
+        load(("x", 0, 0))
+        load(("z", 0, 1))
+        load(("w", 0, 4))
+        constants_turn()
+        load(("w", 0, 3))
+        sign_w(("w", 0, 0))
+        load(("z", 0, 2))
+        interleave(("s", 0, 0), 0, 256, True)
+        interleave(("s", 0, 0), 256, 512, False)
+        interleave(("w", 0, 0), 0, 256, False)
+        interleave(("w", 0, 0), 256, 512, True)
+        bias_load()
+        turn_z(("z", 0, 5), 0)
+        quantize(("s", 0, 0))
+        turn_z(("z", 0, 5), 1)
+        encode(("z", 0, 5), 0)
+        quantize(("w", 0, 0))
+        load(("s", 1, 0))
+        sign_w(("w", 0, 1))
+        encode(("z", 0, 5), 1)
+        interleave(("w", 0, 1), 0, 256, False)
+        load(("z", 0, 4))
+        turn_z(("z", 0, 0), 0)
+        turn_z(("z", 0, 0), 1)
+        interleave(("w", 0, 1), 256, 512, False)
+        encode(("z", 0, 0), 0)
+        interleave(("z", 0, 5), 0, 256, False)
+        load(("z", 1, 0))
+        turn_x(("x", 0, 0), 0)
+        interleave(("z", 0, 5), 256, 512, False)
+        turn_x(("x", 0, 0), 1)
+        encode(("z", 0, 0), 1)
+        quantize(("w", 0, 1))
+        load(("w", 0, 2))
+        turn_z(("z", 0, 1), 0)
+        quantize(("z", 0, 5))
+        copy_words(("x", 0, 0), 0, True)
+        turn_z(("z", 0, 1), 1)
+        interleave(("z", 0, 0), 0, 256, False)
+        copy_words(("x", 0, 0), 1, True)
+        load(("z", 0, 3))
+        interleave(("z", 0, 0), 256, 512, False)
+        encode(("z", 0, 1), 0)
+        quantize(("x", 0, 0))
+        quantize(("z", 0, 0))
+        encode(("z", 0, 1), 1)
+        load(("z", 1, 2))
+        skip(0, 3, 0)
+        sign_w(("w", 0, 4))
+        skip(0, 1, 0)
+        decode(0, 3, 0, 0)
+        decode(0, 2, 0, 0)
+        sign_w(("w", 0, 3))
+        interleave(("w", 0, 4), 0, 256, True)
+        skip(0, 0, 0)
+        load(("w", 1, 2))
+        decode(0, 0, 0, 0)
+        interleave(("z", 0, 1), 0, 256, False)
+        skip(0, 2, 0)
+        turn_z(("z", 0, 2), 0)
+        interleave(("z", 0, 1), 256, 512, False)
+        interleave(("w", 0, 4), 256, 512, True)
+        interleave(("w", 0, 3), 0, 256, False)
+        add_bias(3, 0)
+        encode(("z", 0, 2), 0)
+        load(("x", 1, 0))
+        add_bias(1, 0)
+        turn_z(("z", 0, 2), 1)
+        add_bias(0, 0)
+        interleave(("w", 0, 3), 256, 512, True)
+        load(("w", 0, 5))
+        decode(0, 1, 0, 0)
+        quantize(("z", 0, 1))
+        quantize(("w", 0, 4))
+        decode(0, 3, 0, 1)
+        encode(("z", 0, 2), 1)
+        decode(0, 2, 0, 1)
+        interleave(("s", 1, 0), 0, 256, False)
+        load(("z", 1, 4))
+        decode(0, 0, 0, 1)
+        decode(0, 1, 0, 1)
+        quantize(("w", 0, 3))
+        turn_z(("z", 0, 4), 0)
+        interleave(("s", 1, 0), 256, 512, True)
+        add_bias(2, 0)
+        turn_z(("z", 0, 4), 1)
+        interleave(("z", 0, 2), 0, 256, False)
+        turn_z(("z", 1, 0), 0)
+        encode(("z", 0, 4), 0)
+        interleave(("z", 0, 2), 256, 512, False)
+        turn_z(("z", 1, 0), 1)
+        load(("z", 1, 1))
+        load(("w", 1, 0))
+        quantize(("s", 1, 0))
+        encode(("z", 0, 4), 1)
+        quantize(("z", 0, 2))
+        skip(0, 0, 1)
+        load(("z", 1, 3))
+        sign_w(("w", 0, 2))
+        encode(("z", 1, 0), 0)
+        add_bias(0, 1)
+        turn_z(("z", 0, 3), 0)
+        interleave(("z", 0, 4), 0, 256, False)
+        encode(("z", 1, 0), 1)
+        interleave(("z", 0, 4), 256, 512, False)
+        turn_z(("z", 0, 3), 1)
+        interleave(("w", 0, 2), 0, 256, False)
+        turn_z(("z", 1, 2), 0)
+        load(("w", 1, 1))
+        encode(("z", 0, 3), 0)
+        quantize(("z", 0, 4))
+        turn_z(("z", 1, 2), 1)
+        interleave(("z", 1, 0), 0, 256, False)
+        load(("z", 1, 5))
+        encode(("z", 0, 3), 1)
+        interleave(("z", 1, 0), 256, 512, False)
+        turn_x(("x", 1, 0), 0)
+        interleave(("w", 0, 2), 256, 512, False)
+        encode(("z", 1, 2), 0)
+        turn_x(("x", 1, 0), 1)
+        quantize(("z", 1, 0))
+        load(("w", 1, 3))
+        quantize(("w", 0, 2))
+        load(("x", 2, 0))
+        encode(("z", 1, 2), 1)
+        decode(1, 4, 0, 0)
+        interleave(("z", 0, 3), 0, 256, False)
+        decode(0, 3, 0, 2)
+        interleave(("z", 0, 3), 256, 512, False)
+        decode(0, 2, 0, 2)
+        copy_words(("x", 1, 0), 0, True)
+        decode(0, 0, 0, 2)
+        decode(0, 1, 0, 2)
+        interleave(("z", 1, 2), 0, 256, False)
+        copy_words(("x", 1, 0), 1, True)
+        skip(0, 1, 1)
+        turn_z(("z", 1, 4), 0)
+        quantize(("z", 0, 3))
+        interleave(("z", 1, 2), 256, 512, True)
+        turn_z(("z", 1, 4), 1)
+        sign_w(("w", 1, 2))
+        decode(0, 3, 0, 3)
+        quantize(("x", 1, 0))
+        load(("w", 1, 4))
+        encode(("z", 1, 4), 0)
+        decode(0, 3, 0, 4)
+        decode(0, 2, 0, 3)
+        quantize(("z", 1, 2))
+        decode(0, 2, 0, 4)
+        decode(0, 0, 0, 3)
+        interleave(("w", 1, 2), 0, 256, False)
+        decode(0, 0, 0, 4)
+        encode(("z", 1, 4), 1)
+        skip(1, 7, 0)
+        interleave(("w", 1, 2), 256, 512, False)
+        decode(0, 1, 0, 3)
+        decode(0, 1, 0, 4)
+        add_bias(7, 0)
+        load(("z", 2, 3))
+        skip(1, 6, 1)
+        interleave(("z", 1, 4), 0, 256, True)
+        quantize(("w", 1, 2))
+        turn_z(("z", 1, 1), 0)
+        add_bias(6, 1)
+        interleave(("z", 1, 4), 256, 512, True)
+        add_bias(1, 1)
+        skip(1, 5, 0)
+        sign_w(("w", 0, 5))
+        turn_z(("z", 1, 1), 1)
+        add_bias(5, 0)
+        encode(("z", 1, 1), 0)
+        interleave(("w", 0, 5), 0, 256, False)
+        load(("w", 1, 5))
+        turn_z(("z", 1, 3), 0)
+        interleave(("w", 0, 5), 256, 512, False)
+        encode(("z", 1, 1), 1)
+        turn_z(("z", 1, 3), 1)
+        quantize(("z", 1, 4))
+        load(("z", 2, 2))
+        load(("z", 2, 5))
+        quantize(("w", 0, 5))
+        encode(("z", 1, 3), 0)
+        turn_z(("z", 1, 5), 0)
+        interleave(("z", 1, 1), 0, 256, False)
+        decode(0, 3, 0, 5)
+        interleave(("z", 1, 1), 256, 512, False)
+        decode(0, 2, 0, 5)
+        encode(("z", 1, 3), 1)
+        decode(0, 0, 0, 5)
+        decode(0, 1, 0, 5)
+        finish(3, 0)
+        decode(1, 5, 0, 0)
+        finish(2, 0)
+        encode(("z", 1, 5), 0)
+        store_y(3, 0)
+        decode(1, 6, 0, 0)
+        skip(1, 4, 0)
+        finish(0, 0)
+        store_y(2, 0)
+        decode(1, 7, 0, 0)
+        round_y(2, 0, False)
+        round_y(3, 0, True)
+        store_y(0, 0)
+        round_y(0, 0, False)
+        skip(0, 2, 1)
+        turn_z(("z", 1, 5), 1)
+        finish(1, 0)
+        interleave(("z", 1, 3), 0, 256, True)
+        quantize(("z", 1, 1))
+        turn_x(("x", 2, 0), 0)
+        store_y(1, 0)
+        load(("z", 2, 0))
+        sign_w(("w", 1, 0))
+        round_y(1, 0, True)
+        decode(1, 4, 0, 1)
+        load(("z", 2, 1))
+        interleave(("z", 1, 3), 256, 512, False)
+        decode(1, 4, 0, 2)
+        encode(("z", 1, 5), 1)
+        decode(1, 5, 0, 1)
+        decode(1, 5, 0, 2)
+        interleave(("w", 1, 0), 0, 256, False)
+        decode(1, 6, 0, 1)
+        decode(1, 6, 0, 2)
+        interleave(("w", 1, 0), 256, 512, False)
+        copy_words(("x", 2, 0), 0, True)
+        decode(1, 7, 0, 1)
+        decode(1, 7, 0, 2)
+        quantize(("z", 1, 3))
+        skip(1, 6, 0)
+        interleave(("z", 1, 5), 0, 256, True)
+        load(("z", 2, 4))
+        turn_y(("y", 0, 0), 0)
+        quantize(("w", 1, 0))
+        decode(1, 4, 0, 3)
+        add_bias(4, 0)
+        decode(1, 4, 0, 4)
+        copy_words(("y", 0, 0), 0, True)
+        decode(1, 5, 0, 3)
+        sign_w(("w", 1, 1))
+        decode(1, 5, 0, 4)
+        interleave(("z", 1, 5), 256, 512, True)
+        decode(1, 5, 1, 0)
+        decode(1, 6, 0, 3)
+        add_bias(2, 1)
+        decode(1, 6, 0, 4)
+        decode(1, 7, 0, 3)
+        interleave(("w", 1, 1), 0, 256, False)
+        interleave(("w", 1, 1), 256, 512, True)
+        decode(1, 7, 0, 4)
+        skip(1, 4, 1)
+        quantize(("z", 1, 5))
+        turn_z(("z", 2, 3), 0)
+        sign_w(("w", 1, 3))
+        decode(1, 4, 0, 5)
+        encode(("z", 2, 3), 0)
+        quantize(("w", 1, 1))
+        decode(1, 5, 0, 5)
+        decode(1, 6, 0, 5)
+        interleave(("w", 1, 3), 0, 256, True)
+        decode(1, 7, 0, 5)
+        finish(5, 0)
+        decode(1, 5, 1, 1)
+        decode(1, 5, 1, 2)
+        finish(4, 0)
+        store_y(5, 0)
+        decode(1, 6, 1, 0)
+        round_y(5, 0, True)
+        decode(1, 6, 1, 1)
+        interleave(("w", 1, 3), 256, 512, False)
+        store_y(4, 0)
+        decode(1, 6, 1, 2)
+        round_y(4, 0, True)
+        decode(0, 1, 1, 0)
+        add_bias(6, 0)
+        decode(0, 1, 1, 1)
+        decode(0, 1, 1, 2)
+        quantize(("w", 1, 3))
+        turn_y(("y", 1, 0), 0)
+        finish(6, 0)
+        decode(0, 0, 1, 0)
+        copy_words(("y", 1, 0), 0, True)
+        decode(1, 5, 1, 3)
+        quantize(("x", 2, 0))
+        decode(1, 6, 1, 3)
+        store_y(6, 0)
+        sign_w(("w", 1, 4))
+        round_y(6, 0, True)
+        decode(0, 1, 1, 3)
+        decode(0, 0, 1, 1)
+        sign_w(("w", 1, 5))
+        decode(0, 0, 1, 2)
+        interleave(("w", 1, 4), 0, 256, True)
+        decode(0, 0, 1, 3)
+        interleave(("w", 1, 4), 256, 512, False)
+        skip(2, 9, 1)
+        turn_z(("z", 2, 3), 1)
+        add_bias(9, 1)
+        interleave(("w", 1, 5), 0, 256, True)
+        quantize(("w", 1, 4))
+        turn_y(("y", 0, 0), 1)
+        interleave(("w", 1, 5), 256, 512, False)
+        decode(1, 5, 1, 4)
+        encode(("z", 2, 3), 1)
+        decode(1, 6, 1, 4)
+        add_bias(4, 1)
+        decode(0, 1, 1, 4)
+        copy_words(("y", 0, 0), 1, True)
+        decode(0, 0, 1, 4)
+        quantize(("w", 1, 5))
+        skip(2, 8, 0)
+        interleave(("z", 2, 3), 0, 256, True)
+        skip(2, 8, 1)
+        finish(7, 0)
+        decode(1, 5, 1, 5)
+        decode(1, 6, 1, 5)
+        add_bias(8, 0)
+        store_y(7, 0)
+        decode(0, 1, 1, 5)
+        round_y(7, 0, True)
+        decode(0, 0, 1, 5)
+        add_bias(8, 1)
+        decode(0, 3, 1, 0)
+        decode(0, 3, 1, 1)
+        quantize(("z", 2, 3))
+        decode(0, 3, 1, 2)
+        quantize_y(("y", 0, 0))
+        decode(0, 3, 1, 3)
+        decode(0, 3, 1, 4)
+        finish(6, 1)
+        decode(0, 3, 1, 5)
+        store_words(("y", 0, 0))
+        skip(2, 9, 0)
+        finish(1, 1)
+        decode(1, 7, 1, 0)
+        store_y(6, 1)
+        round_y(6, 1, True)
+        decode(1, 7, 1, 1)
+        add_bias(9, 0)
+        decode(1, 7, 1, 2)
+        store_y(1, 1)
+        round_y(1, 1, True)
+        decode(1, 7, 1, 3)
+        finish(0, 1)
+        decode(1, 7, 1, 4)
+        decode(1, 7, 1, 5)
+        skip(1, 7, 1)
+        store_y(0, 1)
+        skip(0, 3, 1)
+        turn_z(("z", 2, 2), 0)
+        add_bias(7, 1)
+        turn_z(("z", 2, 2), 1)
+        add_bias(3, 1)
+        turn_z(("z", 2, 5), 0)
+        encode(("z", 2, 2), 0)
+        turn_z(("z", 2, 5), 1)
+        finish(7, 1)
+        encode(("z", 2, 2), 1)
+        turn_z(("z", 2, 0), 0)
+        turn_z(("z", 2, 0), 1)
+        finish(3, 1)
+        turn_y(("y", 1, 0), 1)
+        store_y(7, 1)
+        encode(("z", 2, 5), 0)
+        turn_z(("z", 2, 1), 0)
+        interleave(("z", 2, 2), 0, 256, False)
+        store_y(3, 1)
+        turn_z(("z", 2, 1), 1)
+        round_y(7, 1, True)
+        round_y(3, 1, False)
+        decode(1, 4, 1, 0)
+        quantize(("z", 2, 2))
+        encode(("z", 2, 5), 1)
+        decode(1, 4, 1, 1)
+        copy_words(("y", 1, 0), 1, False)
+        decode(1, 4, 1, 2)
+        decode(1, 4, 1, 3)
+        encode(("z", 2, 0), 0)
+        decode(1, 4, 1, 4)
+        interleave(("z", 2, 5), 0, 256, False)
+        turn_y(("y", 1, 1), 1)
+        encode(("z", 2, 0), 1)
+        quantize_y(("y", 1, 0))
+        decode(1, 4, 1, 5)
+        copy_words(("y", 1, 1), 1, True)
+        decode(0, 2, 1, 0)
+        quantize(("z", 2, 5))
+        decode(0, 2, 1, 1)
+        store_words(("y", 1, 0))
+        finish(4, 1)
+        encode(("z", 2, 1), 0)
+        decode(0, 2, 1, 2)
+        decode(0, 2, 1, 3)
+        interleave(("z", 2, 0), 0, 256, False)
+        decode(0, 2, 1, 4)
+        store_y(4, 1)
+        round_y(4, 1, True)
+        decode(0, 2, 1, 5)
+        round_y(0, 1, False)
+        turn_z(("z", 2, 4), 0)
+        encode(("z", 2, 1), 1)
+        quantize(("z", 2, 0))
+        turn_z(("z", 2, 4), 1)
+        finish(2, 1)
+        turn_y(("y", 0, 1), 0)
+        encode(("z", 2, 4), 0)
+        decode(2, 8, 0, 0)
+        interleave(("z", 2, 1), 0, 256, False)
+        store_y(2, 1)
+        decode(2, 9, 0, 0)
+        copy_words(("y", 0, 1), 0, True)
+        decode(2, 8, 1, 0)
+        round_y(2, 1, False)
+        decode(2, 9, 1, 0)
+        encode(("z", 2, 4), 1)
+        quantize(("z", 2, 1))
+        skip(1, 5, 1)
+        turn_y(("y", 0, 1), 1)
+        add_bias(5, 1)
+        interleave(("z", 2, 4), 0, 256, True)
+        decode(2, 8, 0, 1)
+        copy_words(("y", 0, 1), 1, False)
+        decode(2, 8, 0, 2)
+        decode(2, 8, 0, 3)
+        finish(5, 1)
+        decode(2, 9, 0, 1)
+        decode(2, 9, 0, 2)
+        quantize_y(("y", 0, 1))
+        decode(2, 9, 0, 3)
+        store_y(5, 1)
+        round_y(5, 1, True)
+        decode(2, 8, 1, 1)
+        decode(2, 8, 1, 2)
+        quantize(("z", 2, 4))
+        store_words(("y", 0, 1))
+        decode(2, 8, 1, 3)
+        decode(2, 8, 0, 4)
+        decode(2, 8, 0, 5)
+        decode(2, 9, 0, 4)
+        decode(2, 9, 0, 5)
+        finish(8, 0)
+        decode(2, 8, 1, 4)
+        decode(2, 8, 1, 5)
+        finish(9, 0)
+        store_y(8, 0)
+        round_y(8, 0, True)
+        decode(2, 9, 1, 1)
+        decode(2, 9, 1, 2)
+        finish(8, 1)
+        store_y(9, 0)
+        decode(2, 9, 1, 3)
+        round_y(9, 0, True)
+        decode(2, 9, 1, 4)
+        store_y(8, 1)
+        decode(2, 9, 1, 5)
+        turn_y(("y", 1, 1), 0)
+        finish(9, 1)
+        turn_y(("y", 2, 0), 0)
+        copy_words(("y", 1, 1), 0, True)
+        round_y(8, 1, False)
+        store_y(9, 1)
+        round_y(9, 1, False)
+        copy_words(("y", 2, 0), 0, True)
+        quantize_y(("y", 1, 1))
+        turn_y(("y", 2, 1), 0)
+        quantize_y(("y", 2, 0))
+        copy_words(("y", 2, 1), 0, True)
+        store_words(("y", 1, 1))
+        store_words(("y", 2, 0))
+        store_scales(0)
+        quantize_y(("y", 2, 1))
+        store_words(("y", 2, 1))
+        store_scales(1)

@@ -44,7 +44,6 @@ def tile_sae_relu_decode_skip_g1_kernel(tc, pre, b_enc, g, w_dec, b_dec, r, x, w
         y_scales = [keep.tile([P, M], U8, name="y_scales%d" % n, align_bytes=64) for n in range(2)]
 
         raw, slots, grouped, codes, scales, banks, part, ybf = {}, {}, {}, {}, {}, {}, {}, {}
-
         free_banks = list(range(8))
         held = {}
 
@@ -59,30 +58,47 @@ def tile_sae_relu_decode_skip_g1_kernel(tc, pre, b_enc, g, w_dec, b_dec, r, x, w
         def width(u):
             return CHUNKS[u[1]][1] * P if u[0] in "zxy" else HALF
 
+        def move(engine, dst, src):
+            if engine == "A":
+                nc.scalar.copy(out=dst, in_=src)
+            elif engine == "V":
+                nc.vector.tensor_copy(out=dst, in_=src)
+            else:
+                nc.gpsimd.tensor_scalar(out=dst, in0=src, scalar1=1.0, scalar2=-0.0, op0=ALU.mult, op1=ALU.add)
+
         def constants_load():
-            nc.vector.memset(vec_rows[:], 0.0)
+            nc.vector.memset(vec_rows[:].bitcast(U32), 0)
             make_identity(nc, ident[:])
-            nc.scalar.dma_start(out=vec_rows[0:G, :], in_=g.rearrange("(c k) -> c k", k=KP))
-            nc.scalar.dma_start(out=vec_rows[B_ROW:B_ROW + G, :], in_=b_enc.rearrange("(c k) -> c k", k=KP))
-            nc.scalar.dma_start(out=vec_rows[R_ROW:R_ROW + M // P, 0:P], in_=r.rearrange("(m p) o -> m (p o)", p=P))
-            nc.vector.tensor_copy(out=ident_bf[:], in_=ident[:])
+            for vec, row in ((g, 0), (b_enc, B_ROW)):
+                rows = vec.rearrange("(c k) -> c k", k=KP)
+                nc.sync.dma_start(out=vec_rows[row:row + 4, :], in_=rows[0:4])
+                nc.sync.dma_start(out=vec_rows[row + 4:row + G, :], in_=rows[4:G])
+            nc.scalar.copy(out=ident_bf[:], in_=ident[:])
 
         def constants_turn():
             bank = take("vec", [P, 2, P], F32)
-            words = vec_rows[:].bitcast(F32)
-            for u in range(2):
-                nc.tensor.transpose(bank[:, u, :], words[:, u::2], ident[:])
-            r_bank = take("r", [P, P], BF16)
-            nc.tensor.transpose(r_bank[:], vec_rows[:, 0:P], ident_bf[:])
-            vals = bank[:].rearrange("p u c -> p (u c)").bitcast(BF16).rearrange("p (u c e) -> p c u e", u=2, e=2)
+            for h in range(2):
+                nc.tensor.transpose(bank[:, h, :], vec_rows[:].bitcast(F32)[:, h::2], ident[:])
+
+        def constants_make():
+            vals = banks["vec"][:].rearrange("p h c -> p (h c)").bitcast(BF16).rearrange("p (h c e) -> p c h e", h=2, e=2)
             g_t, b_t = vals[:, 0:G], vals[:, B_ROW:B_ROW + G]
-            split = lambda t: t[:].rearrange("p c (u e) -> p c u e", e=2)
+            split = lambda t: t[:].rearrange("p c (h e) -> p c h e", e=2)
             nc.vector.tensor_scalar(out=split(sign), in0=g_t, scalar1=0.0, scalar2=2.0, op0=ALU.is_ge, op1=ALU.mult)
             nc.vector.tensor_scalar(out=sign[:], in0=sign[:], scalar1=-1.0, scalar2=None, op0=ALU.add)
             nc.vector.tensor_tensor(out=split(g_abs), in0=g_t, in1=split(sign), op=ALU.mult)
             nc.vector.tensor_tensor(out=split(gb), in0=b_t, in1=split(g_abs), op=ALU.mult)
-            nc.scalar.copy(out=r_col[:], in_=r_bank[:, R_ROW:R_ROW + M // P])
             release("vec")
+
+        def r_load():
+            rows = r.rearrange("(m p) o -> m (p o)", p=P)
+            nc.sync.dma_start(out=vec_rows[R_ROW:R_ROW + M // P, 0:P], in_=rows)
+
+        def r_turn():
+            nc.tensor.transpose(take("r", [P, P], BF16)[:], vec_rows[:, 0:P], ident_bf[:])
+
+        def r_copy():
+            nc.scalar.copy(out=r_col[:], in_=banks["r"][:, R_ROW:R_ROW + M // P])
             release("r")
 
         def bias_load():
@@ -90,7 +106,7 @@ def tile_sae_relu_decode_skip_g1_kernel(tc, pre, b_enc, g, w_dec, b_dec, r, x, w
 
         def load(u):
             kind, a, b = u
-            t = work.tile([P, PACK, KP], BF16, name="raw", tag="raw", bufs=10)
+            t = work.tile([P, PACK, KP], BF16, name="raw", bufs=10)
             raw[u] = t
             if kind in "zx":
                 m0, nm = CHUNKS[a]
@@ -100,42 +116,41 @@ def tile_sae_relu_decode_skip_g1_kernel(tc, pre, b_enc, g, w_dec, b_dec, r, x, w
                 src = (w_dec if kind == "w" else w_skip)[b * KP:(b + 1) * KP, a * HALF:(a + 1) * HALF]
                 nc.sync.dma_start(out=t[:], in_=src.rearrange("(p j) d -> p j d", j=PACK))
 
+        def halves(h):
+            return (0, 1) if h == 2 else (h,)
+
         def turn_z(u, h):
             nm = CHUNKS[u[1]][1]
-            bank = take((u, h), [P, nm * P], F32)
-            for m in range(nm):
-                nc.tensor.transpose(bank[:, m * P:(m + 1) * P], raw[u][:, m, :].bitcast(F32)[:, h::2], ident[:])
+            bank = take((u, h), [P, len(halves(h)), nm * P], F32)
+            for i, hh in enumerate(halves(h)):
+                for m in range(nm):
+                    nc.tensor.transpose(bank[:, i, m * P:(m + 1) * P], raw[u][:, m, :].bitcast(F32)[:, hh::2], ident[:])
 
         def encode(u, h):
             w = width(u)
             if u not in slots:
-                slots[u] = work.tile([P, PACK, KP], BF16, name="slots", tag="slots", bufs=3)
-            t = slots[u]
-            for j in range(2 * h, 2 * h + 2):
-                src = banks[u, j // 2][:].bitcast(BF16)[:, j % 2::2]
-                nc.scalar.activation(out=t[:, j, 0:w], in_=src, func=ACT.Relu,
-                                     bias=gb[:, u[2], j:j + 1], scale=g_abs[:, u[2], j:j + 1])
-                if j % 2:
-                    release((u, j // 2))
+                slots[u] = work.tile([P, PACK, KP], BF16, name="slots", bufs=3)
+            for i, hh in enumerate(halves(h)):
+                for e in range(2):
+                    j = 2 * hh + e
+                    nc.scalar.activation(out=slots[u][:, j, 0:w], in_=banks[u, h][:, i, :].bitcast(BF16)[:, e::2], func=ACT.Relu,
+                                         bias=gb[:, u[2], j:j + 1], scale=g_abs[:, u[2], j:j + 1])
+            release((u, h))
 
         def sign_w(u):
-            slots[u] = raw[u]
             for j in range(PACK):
                 nc.vector.tensor_scalar(out=raw[u][:, j, :], in0=raw[u][:, j, :], scalar1=sign[:, u[2], j:j + 1],
                                         scalar2=None, op0=ALU.mult)
 
         def new_grouped(u):
             if u not in grouped:
-                grouped[u] = work.tile([P, KP * PACK], BF16, name="grouped", tag="grouped", bufs=4, align_bytes=64)
+                grouped[u] = work.tile([P, KP * PACK], BF16, name="grouped", bufs=5, align_bytes=64)
             return grouped[u]
 
-        def interleave(u, c0, c1, on_scalar):
+        def interleave(u, c0, c1, engine):
             src = slots.get(u, raw[u])[:, :, c0:c1].rearrange("p t (c i) -> p c t i", i=4)
             dst = new_grouped(u)[:, c0 * PACK:c1 * PACK].rearrange("p (c i t) -> p c t i", i=4, t=PACK)
-            if on_scalar:
-                nc.scalar.copy(out=dst, in_=src)
-            else:
-                nc.vector.tensor_copy(out=dst, in_=src)
+            move(engine, dst, src)
 
         def quantize(u):
             w = width(u)
@@ -157,13 +172,9 @@ def tile_sae_relu_decode_skip_g1_kernel(tc, pre, b_enc, g, w_dec, b_dec, r, x, w
             m0 = CHUNKS[u[1]][0]
             turn_words(u, pair, lambda m, h: ybf[m0 + m, u[2]][:].bitcast(F32)[:, h * P:(h + 1) * P])
 
-        def copy_words(u, pair, on_scalar):
+        def copy_words(u, pair, engine):
             dst = new_grouped(u)[:].bitcast(F32)[:, pair * KP:(pair + 1) * KP].rearrange("p (m c h) -> p m c h", m=2, h=2)
-            src = banks[u, pair][:].rearrange("p m h c -> p m c h")
-            if on_scalar:
-                nc.scalar.copy(out=dst, in_=src)
-            else:
-                nc.vector.tensor_copy(out=dst, in_=src)
+            move(engine, dst, banks[u, pair][:].rearrange("p m h c -> p m c h"))
             release((u, pair))
 
         def mx(out, a, m, b, start, stop):
@@ -179,9 +190,12 @@ def tile_sae_relu_decode_skip_g1_kernel(tc, pre, b_enc, g, w_dec, b_dec, r, x, w
         def skip(c, m, n):
             mx(take(("skip", m, n), [P, HALF], F32), ("x", c, 0), m, ("s", n, 0), True, True)
 
+        def new_y(m, n):
+            part[m, n] = work.tile([P, HALF], F32, name="y", bufs=18)
+            return part[m, n]
+
         def add_bias(m, n):
-            part[m, n] = work.tile([P, HALF], F32, name="y", tag="y", bufs=10)
-            nc.vector.scalar_tensor_tensor(out=part[m, n][:], in0=b_all[:, n * HALF:(n + 1) * HALF], scalar=r_col[:, m:m + 1],
+            nc.vector.scalar_tensor_tensor(out=new_y(m, n)[:], in0=b_all[:, n * HALF:(n + 1) * HALF], scalar=r_col[:, m:m + 1],
                                            in1=banks["skip", m, n][:], op0=ALU.mult, op1=ALU.add)
             release(("skip", m, n))
 
@@ -191,29 +205,34 @@ def tile_sae_relu_decode_skip_g1_kernel(tc, pre, b_enc, g, w_dec, b_dec, r, x, w
                                            op0=ALU.mult, op1=ALU.add)
             release(("acc", m, n))
 
+        def bias_first(m, n):
+            nc.vector.tensor_tensor(out=new_y(m, n)[:], in0=banks["acc", m, n][:], in1=b_all[:, n * HALF:(n + 1) * HALF], op=ALU.add)
+            release(("acc", m, n))
+
+        def skip_last(m, n):
+            y = part[m, n]
+            nc.vector.scalar_tensor_tensor(out=y[:], in0=y[:], scalar=r_col[:, m:m + 1], in1=banks["skip", m, n][:],
+                                           op0=ALU.mult, op1=ALU.add)
+            release(("skip", m, n))
+
         def store_y(m, n):
             nc.sync.dma_start(out=out_0[m * P:(m + 1) * P, n * HALF:(n + 1) * HALF], in_=part[m, n][:])
 
-        def round_y(m, n, on_scalar):
-            ybf[m, n] = work.tile([P, HALF], BF16, name="ybf", tag="ybf", bufs=4)
+        def round_y(m, n, engine):
+            ybf[m, n] = work.tile([P, HALF], BF16, name="ybf", bufs=6)
             dst = ybf[m, n][:].rearrange("p (h q e) -> p h q e", h=2, e=2)
-            src = part[m, n][:].rearrange("p (q h e) -> p h q e", h=2, e=2)
-            if on_scalar:
-                nc.scalar.copy(out=dst, in_=src)
-            else:
-                nc.vector.tensor_copy(out=dst, in_=src)
+            move(engine, dst, part[m, n][:].rearrange("p (q h e) -> p h q e", h=2, e=2))
+
+        def token_cols(u):
+            return slice(CHUNKS[u[1]][0] * P, CHUNKS[u[1]][0] * P + width(u))
 
         def quantize_y(u):
-            c, n = u[1], u[2]
-            cols = slice(CHUNKS[c][0] * P, CHUNKS[c][0] * P + width(u))
-            nc.vector.quantize_mx(out=y_codes[n][:, cols].bitcast(FP8X4), scales=y_scales[n][:, cols],
+            nc.vector.quantize_mx(out=y_codes[u[2]][:, token_cols(u)].bitcast(FP8X4), scales=y_scales[u[2]][:, token_cols(u)],
                                   in_=grouped[u][:, 0:width(u) * PACK])
 
         def store_words(u):
-            c, n = u[1], u[2]
-            cols = slice(CHUNKS[c][0] * P, CHUNKS[c][0] * P + width(u))
-            dst = out_1[n].rearrange("p m t -> p (m t)").bitcast(I32)
-            nc.sync.dma_start(out=dst[:, cols], in_=y_codes[n][:, cols].bitcast(I32))
+            dst = out_1[u[2]].rearrange("p m t -> p (m t)").bitcast(I32)
+            nc.sync.dma_start(out=dst[:, token_cols(u)], in_=y_codes[u[2]][:, token_cols(u)].bitcast(I32))
 
         def store_scales(n):
             for q in range(4):
@@ -221,482 +240,463 @@ def tile_sae_relu_decode_skip_g1_kernel(tc, pre, b_enc, g, w_dec, b_dec, r, x, w
                 eng.dma_start(out=out_2[n, 4 * q:4 * q + 4, :].bitcast(I32),
                               in_=y_scales[n][32 * q:32 * q + 4, :].bitcast(I32))
 
-        constants_load()
-        load(("w", 0, 0))
         load(("s", 0, 0))
-        load(("z", 0, 5))
-        load(("w", 0, 1))
-        load(("z", 0, 0))
+        constants_load()
         load(("x", 0, 0))
-        load(("z", 0, 1))
-        load(("w", 0, 4))
-        constants_turn()
+        load(("w", 0, 1))
+        load(("w", 0, 0))
+        load(("w", 0, 2))
+        load(("z", 0, 0))
         load(("w", 0, 3))
-        sign_w(("w", 0, 0))
+        load(("z", 0, 1))
         load(("z", 0, 2))
-        interleave(("s", 0, 0), 0, 256, True)
-        interleave(("s", 0, 0), 256, 512, False)
-        interleave(("w", 0, 0), 0, 256, False)
-        interleave(("w", 0, 0), 256, 512, True)
-        bias_load()
-        turn_z(("z", 0, 5), 0)
+        interleave(("s", 0, 0), 0, 256, "V")
+        interleave(("s", 0, 0), 256, 512, "A")
+        constants_turn()
+        constants_make()
+        load(("x", 2, 0))
+        turn_x(("x", 0, 0), 0)
         quantize(("s", 0, 0))
-        turn_z(("z", 0, 5), 1)
-        encode(("z", 0, 5), 0)
-        quantize(("w", 0, 0))
-        load(("s", 1, 0))
+        turn_x(("x", 0, 0), 1)
+        copy_words(("x", 0, 0), 0, "A")
         sign_w(("w", 0, 1))
-        encode(("z", 0, 5), 1)
-        interleave(("w", 0, 1), 0, 256, False)
-        load(("z", 0, 4))
+        load(("w", 0, 4))
+        copy_words(("x", 0, 0), 1, "A")
+        quantize(("x", 0, 0))
+        interleave(("w", 0, 1), 0, 256, "A")
+        load(("z", 1, 1))
+        sign_w(("w", 0, 0))
+        interleave(("w", 0, 1), 256, 512, "V")
+        interleave(("w", 0, 0), 0, 512, "A")
+        r_load()
+        sign_w(("w", 0, 2))
+        quantize(("w", 0, 1))
+        interleave(("w", 0, 2), 0, 512, "V")
+        load(("z", 1, 0))
         turn_z(("z", 0, 0), 0)
         turn_z(("z", 0, 0), 1)
-        interleave(("w", 0, 1), 256, 512, False)
         encode(("z", 0, 0), 0)
-        interleave(("z", 0, 5), 0, 256, False)
-        load(("z", 1, 0))
-        turn_x(("x", 0, 0), 0)
-        interleave(("z", 0, 5), 256, 512, False)
-        turn_x(("x", 0, 0), 1)
+        quantize(("w", 0, 0))
+        load(("w", 0, 5))
+        quantize(("w", 0, 2))
         encode(("z", 0, 0), 1)
-        quantize(("w", 0, 1))
-        load(("w", 0, 2))
-        turn_z(("z", 0, 1), 0)
-        quantize(("z", 0, 5))
-        copy_words(("x", 0, 0), 0, True)
-        turn_z(("z", 0, 1), 1)
-        interleave(("z", 0, 0), 0, 256, False)
-        copy_words(("x", 0, 0), 1, True)
+        sign_w(("w", 0, 3))
         load(("z", 0, 3))
-        interleave(("z", 0, 0), 256, 512, False)
+        turn_z(("z", 0, 1), 0)
+        turn_z(("z", 0, 1), 1)
+        interleave(("z", 0, 0), 0, 256, "V")
+        interleave(("z", 0, 0), 256, 512, "A")
+        interleave(("w", 0, 3), 0, 512, "V")
+        load(("z", 1, 2))
+        turn_z(("z", 0, 2), 0)
+        turn_z(("z", 0, 2), 1)
         encode(("z", 0, 1), 0)
-        quantize(("x", 0, 0))
+        load(("z", 1, 3))
+        turn_x(("x", 2, 0), 0)
         quantize(("z", 0, 0))
         encode(("z", 0, 1), 1)
-        load(("z", 1, 2))
-        skip(0, 3, 0)
-        sign_w(("w", 0, 4))
-        skip(0, 1, 0)
-        decode(0, 3, 0, 0)
-        decode(0, 2, 0, 0)
-        sign_w(("w", 0, 3))
-        interleave(("w", 0, 4), 0, 256, True)
-        skip(0, 0, 0)
-        load(("w", 1, 2))
-        decode(0, 0, 0, 0)
-        interleave(("z", 0, 1), 0, 256, False)
-        skip(0, 2, 0)
-        turn_z(("z", 0, 2), 0)
-        interleave(("z", 0, 1), 256, 512, False)
-        interleave(("w", 0, 4), 256, 512, True)
-        interleave(("w", 0, 3), 0, 256, False)
-        add_bias(3, 0)
-        encode(("z", 0, 2), 0)
-        load(("x", 1, 0))
-        add_bias(1, 0)
-        turn_z(("z", 0, 2), 1)
-        add_bias(0, 0)
-        interleave(("w", 0, 3), 256, 512, True)
-        load(("w", 0, 5))
-        decode(0, 1, 0, 0)
-        quantize(("z", 0, 1))
-        quantize(("w", 0, 4))
-        decode(0, 3, 0, 1)
-        encode(("z", 0, 2), 1)
-        decode(0, 2, 0, 1)
-        interleave(("s", 1, 0), 0, 256, False)
-        load(("z", 1, 4))
-        decode(0, 0, 0, 1)
-        decode(0, 1, 0, 1)
         quantize(("w", 0, 3))
-        turn_z(("z", 0, 4), 0)
-        interleave(("s", 1, 0), 256, 512, True)
-        add_bias(2, 0)
-        turn_z(("z", 0, 4), 1)
-        interleave(("z", 0, 2), 0, 256, False)
-        turn_z(("z", 1, 0), 0)
-        encode(("z", 0, 4), 0)
-        interleave(("z", 0, 2), 256, 512, False)
-        turn_z(("z", 1, 0), 1)
-        load(("z", 1, 1))
-        load(("w", 1, 0))
-        quantize(("s", 1, 0))
-        encode(("z", 0, 4), 1)
-        quantize(("z", 0, 2))
-        skip(0, 0, 1)
-        load(("z", 1, 3))
-        sign_w(("w", 0, 2))
-        encode(("z", 1, 0), 0)
-        add_bias(0, 1)
-        turn_z(("z", 0, 3), 0)
-        interleave(("z", 0, 4), 0, 256, False)
-        encode(("z", 1, 0), 1)
-        interleave(("z", 0, 4), 256, 512, False)
-        turn_z(("z", 0, 3), 1)
-        interleave(("w", 0, 2), 0, 256, False)
-        turn_z(("z", 1, 2), 0)
-        load(("w", 1, 1))
-        encode(("z", 0, 3), 0)
-        quantize(("z", 0, 4))
-        turn_z(("z", 1, 2), 1)
-        interleave(("z", 1, 0), 0, 256, False)
+        load(("z", 0, 4))
+        decode(0, 3, 0, 0)
+        sign_w(("w", 0, 4))
+        decode(0, 0, 0, 0)
+        decode(0, 2, 0, 0)
+        encode(("z", 0, 2), 0)
+        decode(0, 1, 0, 0)
+        interleave(("z", 0, 1), 0, 512, "V")
+        load(("z", 0, 5))
+        turn_z(("z", 1, 1), 0)
         load(("z", 1, 5))
+        encode(("z", 0, 2), 1)
+        r_turn()
+        interleave(("w", 0, 4), 0, 256, "V")
+        bias_load()
+        quantize(("z", 0, 1))
+        r_copy()
+        encode(("z", 1, 1), 0)
+        turn_z(("z", 1, 1), 1)
+        interleave(("z", 0, 2), 0, 256, "V")
+        decode(0, 3, 0, 1)
+        load(("x", 1, 0))
+        decode(0, 0, 0, 1)
+        sign_w(("w", 0, 5))
+        encode(("z", 1, 1), 1)
+        decode(0, 2, 0, 1)
+        decode(0, 1, 0, 1)
+        interleave(("z", 0, 2), 256, 512, "V")
+        turn_z(("z", 1, 0), 0)
+        copy_words(("x", 2, 0), 0, "A")
+        interleave(("w", 0, 4), 256, 512, "V")
+        turn_z(("z", 1, 0), 1)
+        encode(("z", 1, 0), 0)
+        turn_z(("z", 0, 3), 0)
+        quantize(("z", 0, 2))
+        load(("w", 1, 0))
+        turn_z(("z", 0, 3), 1)
+        load(("z", 1, 4))
+        quantize(("x", 2, 0))
+        quantize(("w", 0, 4))
+        encode(("z", 1, 0), 1)
+        decode(0, 3, 0, 2)
+        decode(0, 0, 0, 2)
+        interleave(("z", 1, 1), 0, 512, "V")
+        decode(0, 2, 0, 2)
+        load(("w", 1, 1))
+        decode(0, 1, 0, 2)
+        encode(("z", 0, 3), 0)
+        turn_z(("z", 1, 2), 0)
+        interleave(("z", 1, 0), 0, 256, "V")
+        turn_z(("z", 1, 2), 1)
         encode(("z", 0, 3), 1)
-        interleave(("z", 1, 0), 256, 512, False)
-        turn_x(("x", 1, 0), 0)
-        interleave(("w", 0, 2), 256, 512, False)
+        quantize(("z", 1, 1))
+        turn_z(("z", 1, 3), 0)
+        load(("w", 1, 2))
+        interleave(("z", 1, 0), 256, 512, "V")
         encode(("z", 1, 2), 0)
-        turn_x(("x", 1, 0), 1)
+        turn_z(("z", 1, 3), 1)
+        interleave(("w", 0, 5), 0, 256, "V")
         quantize(("z", 1, 0))
         load(("w", 1, 3))
-        quantize(("w", 0, 2))
-        load(("x", 2, 0))
         encode(("z", 1, 2), 1)
-        decode(1, 4, 0, 0)
-        interleave(("z", 0, 3), 0, 256, False)
-        decode(0, 3, 0, 2)
-        interleave(("z", 0, 3), 256, 512, False)
-        decode(0, 2, 0, 2)
-        copy_words(("x", 1, 0), 0, True)
-        decode(0, 0, 0, 2)
-        decode(0, 1, 0, 2)
-        interleave(("z", 1, 2), 0, 256, False)
-        copy_words(("x", 1, 0), 1, True)
-        skip(0, 1, 1)
-        turn_z(("z", 1, 4), 0)
-        quantize(("z", 0, 3))
-        interleave(("z", 1, 2), 256, 512, True)
-        turn_z(("z", 1, 4), 1)
-        sign_w(("w", 1, 2))
-        decode(0, 3, 0, 3)
-        quantize(("x", 1, 0))
-        load(("w", 1, 4))
-        encode(("z", 1, 4), 0)
-        decode(0, 3, 0, 4)
-        decode(0, 2, 0, 3)
-        quantize(("z", 1, 2))
-        decode(0, 2, 0, 4)
-        decode(0, 0, 0, 3)
-        interleave(("w", 1, 2), 0, 256, False)
-        decode(0, 0, 0, 4)
-        encode(("z", 1, 4), 1)
-        skip(1, 7, 0)
-        interleave(("w", 1, 2), 256, 512, False)
-        decode(0, 1, 0, 3)
-        decode(0, 1, 0, 4)
-        add_bias(7, 0)
-        load(("z", 2, 3))
-        skip(1, 6, 1)
-        interleave(("z", 1, 4), 0, 256, True)
-        quantize(("w", 1, 2))
-        turn_z(("z", 1, 1), 0)
-        add_bias(6, 1)
-        interleave(("z", 1, 4), 256, 512, True)
-        add_bias(1, 1)
-        skip(1, 5, 0)
-        sign_w(("w", 0, 5))
-        turn_z(("z", 1, 1), 1)
-        add_bias(5, 0)
-        encode(("z", 1, 1), 0)
-        interleave(("w", 0, 5), 0, 256, False)
-        load(("w", 1, 5))
-        turn_z(("z", 1, 3), 0)
-        interleave(("w", 0, 5), 256, 512, False)
-        encode(("z", 1, 1), 1)
-        turn_z(("z", 1, 3), 1)
-        quantize(("z", 1, 4))
-        load(("z", 2, 2))
-        load(("z", 2, 5))
-        quantize(("w", 0, 5))
+        turn_z(("z", 0, 4), 0)
+        interleave(("w", 0, 5), 256, 512, "V")
+        interleave(("z", 0, 3), 0, 256, "V")
         encode(("z", 1, 3), 0)
-        turn_z(("z", 1, 5), 0)
-        interleave(("z", 1, 1), 0, 256, False)
-        decode(0, 3, 0, 5)
-        interleave(("z", 1, 1), 256, 512, False)
-        decode(0, 2, 0, 5)
+        load(("w", 1, 4))
+        turn_z(("z", 0, 4), 1)
+        quantize(("w", 0, 5))
+        load(("w", 1, 5))
+        interleave(("z", 0, 3), 256, 512, "V")
         encode(("z", 1, 3), 1)
-        decode(0, 0, 0, 5)
-        decode(0, 1, 0, 5)
-        finish(3, 0)
-        decode(1, 5, 0, 0)
-        finish(2, 0)
-        encode(("z", 1, 5), 0)
-        store_y(3, 0)
-        decode(1, 6, 0, 0)
-        skip(1, 4, 0)
-        finish(0, 0)
-        store_y(2, 0)
-        decode(1, 7, 0, 0)
-        round_y(2, 0, False)
-        round_y(3, 0, True)
-        store_y(0, 0)
-        round_y(0, 0, False)
-        skip(0, 2, 1)
-        turn_z(("z", 1, 5), 1)
-        finish(1, 0)
-        interleave(("z", 1, 3), 0, 256, True)
-        quantize(("z", 1, 1))
-        turn_x(("x", 2, 0), 0)
-        store_y(1, 0)
+        turn_z(("z", 0, 5), 0)
+        interleave(("z", 1, 2), 0, 256, "V")
+        encode(("z", 0, 4), 0)
+        quantize(("z", 0, 3))
+        turn_z(("z", 0, 5), 1)
+        interleave(("z", 1, 2), 256, 512, "V")
+        decode(0, 3, 0, 3)
         load(("z", 2, 0))
+        encode(("z", 0, 4), 1)
+        decode(0, 0, 0, 3)
         sign_w(("w", 1, 0))
-        round_y(1, 0, True)
-        decode(1, 4, 0, 1)
-        load(("z", 2, 1))
-        interleave(("z", 1, 3), 256, 512, False)
-        decode(1, 4, 0, 2)
-        encode(("z", 1, 5), 1)
+        decode(0, 2, 0, 3)
+        decode(0, 1, 0, 3)
+        quantize(("z", 1, 2))
+        decode(1, 5, 0, 0)
+        encode(("z", 0, 5), 0)
         decode(1, 5, 0, 1)
+        interleave(("z", 1, 3), 0, 512, "V")
+        turn_z(("z", 1, 5), 0)
         decode(1, 5, 0, 2)
-        interleave(("w", 1, 0), 0, 256, False)
+        encode(("z", 0, 5), 1)
+        turn_z(("z", 1, 5), 1)
+        interleave(("z", 0, 4), 0, 256, "V")
+        quantize(("z", 1, 3))
+        load(("z", 2, 1))
+        encode(("z", 1, 5), 0)
+        turn_z(("z", 1, 4), 0)
+        sign_w(("w", 1, 1))
+        decode(1, 5, 0, 3)
+        encode(("z", 1, 5), 1)
+        sign_w(("w", 1, 2))
+        turn_z(("z", 1, 4), 1)
+        interleave(("z", 0, 4), 256, 512, "V")
+        load(("z", 2, 2))
+        interleave(("z", 0, 5), 0, 256, "A")
+        sign_w(("w", 1, 3))
+        turn_x(("x", 1, 0), 0)
+        quantize(("z", 0, 4))
+        encode(("z", 1, 4), 0)
+        sign_w(("w", 1, 4))
+        decode(0, 3, 0, 4)
+        decode(0, 0, 0, 4)
+        interleave(("z", 0, 5), 256, 512, "V")
+        decode(0, 2, 0, 4)
+        encode(("z", 1, 4), 1)
+        decode(0, 1, 0, 4)
+        sign_w(("w", 1, 5))
+        turn_x(("x", 1, 0), 1)
+        copy_words(("x", 1, 0), 0, "A")
+        quantize(("z", 0, 5))
+        turn_z(("z", 2, 0), 2)
+        load(("z", 2, 3))
+        copy_words(("x", 1, 0), 1, "A")
+        interleave(("z", 1, 5), 0, 512, "V")
+        turn_z(("z", 2, 1), 2)
+        load(("z", 2, 4))
+        encode(("z", 2, 0), 2)
+        decode(0, 3, 0, 5)
+        load(("z", 2, 5))
+        decode(0, 0, 0, 5)
+        quantize(("x", 1, 0))
+        decode(0, 2, 0, 5)
+        decode(0, 1, 0, 5)
+        encode(("z", 2, 1), 2)
+        bias_first(0, 0)
+        decode(1, 6, 0, 0)
         decode(1, 6, 0, 1)
         decode(1, 6, 0, 2)
-        interleave(("w", 1, 0), 256, 512, False)
-        copy_words(("x", 2, 0), 0, True)
+        bias_first(1, 0)
+        decode(1, 6, 0, 3)
+        decode(1, 7, 0, 0)
+        bias_first(2, 0)
+        interleave(("w", 1, 0), 0, 512, "A")
         decode(1, 7, 0, 1)
         decode(1, 7, 0, 2)
-        quantize(("z", 1, 3))
-        skip(1, 6, 0)
-        interleave(("z", 1, 5), 0, 256, True)
-        load(("z", 2, 4))
-        turn_y(("y", 0, 0), 0)
-        quantize(("w", 1, 0))
-        decode(1, 4, 0, 3)
-        add_bias(4, 0)
-        decode(1, 4, 0, 4)
-        copy_words(("y", 0, 0), 0, True)
-        decode(1, 5, 0, 3)
-        sign_w(("w", 1, 1))
-        decode(1, 5, 0, 4)
-        interleave(("z", 1, 5), 256, 512, True)
-        decode(1, 5, 1, 0)
-        decode(1, 6, 0, 3)
-        add_bias(2, 1)
-        decode(1, 6, 0, 4)
+        bias_first(3, 0)
         decode(1, 7, 0, 3)
-        interleave(("w", 1, 1), 0, 256, False)
-        interleave(("w", 1, 1), 256, 512, True)
-        decode(1, 7, 0, 4)
-        skip(1, 4, 1)
+        decode(1, 4, 0, 0)
         quantize(("z", 1, 5))
-        turn_z(("z", 2, 3), 0)
-        sign_w(("w", 1, 3))
-        decode(1, 4, 0, 5)
-        encode(("z", 2, 3), 0)
-        quantize(("w", 1, 1))
+        decode(1, 4, 0, 1)
+        decode(1, 4, 0, 2)
+        interleave(("z", 1, 4), 0, 512, "V")
+        decode(1, 4, 0, 3)
+        skip(0, 0, 0)
+        turn_z(("z", 2, 2), 2)
+        interleave(("w", 1, 1), 0, 256, "A")
+        load(("s", 1, 0))
+        quantize(("w", 1, 0))
+        turn_z(("z", 2, 3), 2)
+        turn_z(("z", 2, 4), 2)
+        quantize(("z", 1, 4))
+        encode(("z", 2, 2), 2)
+        interleave(("w", 1, 1), 256, 512, "V")
+        decode(1, 5, 0, 4)
         decode(1, 5, 0, 5)
+        interleave(("w", 1, 2), 0, 256, "V")
+        interleave(("w", 1, 2), 256, 512, "A")
+        decode(1, 6, 0, 4)
         decode(1, 6, 0, 5)
-        interleave(("w", 1, 3), 0, 256, True)
-        decode(1, 7, 0, 5)
-        finish(5, 0)
-        decode(1, 5, 1, 1)
-        decode(1, 5, 1, 2)
-        finish(4, 0)
-        store_y(5, 0)
-        decode(1, 6, 1, 0)
-        round_y(5, 0, True)
-        decode(1, 6, 1, 1)
-        interleave(("w", 1, 3), 256, 512, False)
-        store_y(4, 0)
-        decode(1, 6, 1, 2)
-        round_y(4, 0, True)
-        decode(0, 1, 1, 0)
-        add_bias(6, 0)
-        decode(0, 1, 1, 1)
-        decode(0, 1, 1, 2)
-        quantize(("w", 1, 3))
-        turn_y(("y", 1, 0), 0)
-        finish(6, 0)
-        decode(0, 0, 1, 0)
-        copy_words(("y", 1, 0), 0, True)
-        decode(1, 5, 1, 3)
-        quantize(("x", 2, 0))
-        decode(1, 6, 1, 3)
-        store_y(6, 0)
-        sign_w(("w", 1, 4))
-        round_y(6, 0, True)
-        decode(0, 1, 1, 3)
-        decode(0, 0, 1, 1)
-        sign_w(("w", 1, 5))
-        decode(0, 0, 1, 2)
-        interleave(("w", 1, 4), 0, 256, True)
-        decode(0, 0, 1, 3)
-        interleave(("w", 1, 4), 256, 512, False)
-        skip(2, 9, 1)
-        turn_z(("z", 2, 3), 1)
-        add_bias(9, 1)
-        interleave(("w", 1, 5), 0, 256, True)
-        quantize(("w", 1, 4))
-        turn_y(("y", 0, 0), 1)
-        interleave(("w", 1, 5), 256, 512, False)
-        decode(1, 5, 1, 4)
-        encode(("z", 2, 3), 1)
-        decode(1, 6, 1, 4)
-        add_bias(4, 1)
-        decode(0, 1, 1, 4)
-        copy_words(("y", 0, 0), 1, True)
-        decode(0, 0, 1, 4)
-        quantize(("w", 1, 5))
-        skip(2, 8, 0)
-        interleave(("z", 2, 3), 0, 256, True)
-        skip(2, 8, 1)
-        finish(7, 0)
-        decode(1, 5, 1, 5)
-        decode(1, 6, 1, 5)
-        add_bias(8, 0)
-        store_y(7, 0)
-        decode(0, 1, 1, 5)
-        round_y(7, 0, True)
-        decode(0, 0, 1, 5)
-        add_bias(8, 1)
+        bias_first(5, 0)
         decode(0, 3, 1, 0)
-        decode(0, 3, 1, 1)
-        quantize(("z", 2, 3))
-        decode(0, 3, 1, 2)
-        quantize_y(("y", 0, 0))
-        decode(0, 3, 1, 3)
-        decode(0, 3, 1, 4)
-        finish(6, 1)
-        decode(0, 3, 1, 5)
-        store_words(("y", 0, 0))
-        skip(2, 9, 0)
-        finish(1, 1)
-        decode(1, 7, 1, 0)
-        store_y(6, 1)
-        round_y(6, 1, True)
-        decode(1, 7, 1, 1)
-        add_bias(9, 0)
-        decode(1, 7, 1, 2)
-        store_y(1, 1)
-        round_y(1, 1, True)
-        decode(1, 7, 1, 3)
-        finish(0, 1)
-        decode(1, 7, 1, 4)
-        decode(1, 7, 1, 5)
-        skip(1, 7, 1)
-        store_y(0, 1)
-        skip(0, 3, 1)
-        turn_z(("z", 2, 2), 0)
-        add_bias(7, 1)
-        turn_z(("z", 2, 2), 1)
-        add_bias(3, 1)
-        turn_z(("z", 2, 5), 0)
-        encode(("z", 2, 2), 0)
-        turn_z(("z", 2, 5), 1)
-        finish(7, 1)
-        encode(("z", 2, 2), 1)
-        turn_z(("z", 2, 0), 0)
-        turn_z(("z", 2, 0), 1)
-        finish(3, 1)
-        turn_y(("y", 1, 0), 1)
-        store_y(7, 1)
-        encode(("z", 2, 5), 0)
-        turn_z(("z", 2, 1), 0)
-        interleave(("z", 2, 2), 0, 256, False)
-        store_y(3, 1)
-        turn_z(("z", 2, 1), 1)
-        round_y(7, 1, True)
-        round_y(3, 1, False)
-        decode(1, 4, 1, 0)
-        quantize(("z", 2, 2))
-        encode(("z", 2, 5), 1)
-        decode(1, 4, 1, 1)
-        copy_words(("y", 1, 0), 1, False)
-        decode(1, 4, 1, 2)
-        decode(1, 4, 1, 3)
-        encode(("z", 2, 0), 0)
-        decode(1, 4, 1, 4)
-        interleave(("z", 2, 5), 0, 256, False)
-        turn_y(("y", 1, 1), 1)
-        encode(("z", 2, 0), 1)
-        quantize_y(("y", 1, 0))
-        decode(1, 4, 1, 5)
-        copy_words(("y", 1, 1), 1, True)
+        decode(1, 7, 0, 4)
+        bias_first(6, 0)
+        decode(1, 7, 0, 5)
+        interleave(("w", 1, 3), 0, 512, "A")
         decode(0, 2, 1, 0)
-        quantize(("z", 2, 5))
+        quantize(("w", 1, 1))
+        decode(1, 4, 0, 4)
+        decode(1, 4, 0, 5)
+        bias_first(7, 0)
+        decode(0, 1, 1, 0)
+        decode(0, 3, 1, 1)
         decode(0, 2, 1, 1)
-        store_words(("y", 1, 0))
-        finish(4, 1)
-        encode(("z", 2, 1), 0)
+        bias_first(4, 0)
+        decode(0, 1, 1, 1)
+        decode(0, 0, 1, 0)
+        quantize(("w", 1, 2))
+        decode(0, 0, 1, 1)
+        interleave(("w", 1, 4), 0, 256, "A")
+        turn_z(("z", 2, 5), 2)
+        quantize(("w", 1, 3))
+        decode(0, 3, 1, 2)
+        interleave(("w", 1, 4), 256, 512, "V")
+        decode(0, 3, 1, 3)
+        interleave(("w", 1, 5), 0, 256, "A")
         decode(0, 2, 1, 2)
+        interleave(("w", 1, 5), 256, 512, "V")
         decode(0, 2, 1, 3)
-        interleave(("z", 2, 0), 0, 256, False)
+        decode(0, 1, 1, 2)
+        quantize(("w", 1, 4))
+        decode(0, 1, 1, 3)
+        interleave(("z", 2, 0), 0, 256, "A")
+        decode(0, 0, 1, 2)
+        quantize(("w", 1, 5))
+        decode(0, 0, 1, 3)
+        decode(0, 3, 1, 4)
+        skip_last(0, 0)
         decode(0, 2, 1, 4)
-        store_y(4, 1)
-        round_y(4, 1, True)
+        decode(0, 3, 1, 5)
+        interleave(("z", 2, 1), 0, 256, "A")
         decode(0, 2, 1, 5)
-        round_y(0, 1, False)
-        turn_z(("z", 2, 4), 0)
-        encode(("z", 2, 1), 1)
+        interleave(("z", 2, 2), 0, 256, "V")
+        store_y(0, 0)
+        decode(0, 1, 1, 4)
+        decode(0, 1, 1, 5)
+        bias_first(2, 1)
+        decode(0, 0, 1, 4)
+        encode(("z", 2, 3), 2)
+        decode(0, 0, 1, 5)
+        bias_first(1, 1)
+        skip(0, 2, 0)
+        skip(0, 1, 0)
+        bias_first(0, 1)
+        bias_first(3, 1)
+        encode(("z", 2, 4), 2)
+        skip(1, 6, 0)
+        skip(1, 4, 0)
         quantize(("z", 2, 0))
-        turn_z(("z", 2, 4), 1)
-        finish(2, 1)
-        turn_y(("y", 0, 1), 0)
-        encode(("z", 2, 4), 0)
-        decode(2, 8, 0, 0)
-        interleave(("z", 2, 1), 0, 256, False)
-        store_y(2, 1)
-        decode(2, 9, 0, 0)
-        copy_words(("y", 0, 1), 0, True)
-        decode(2, 8, 1, 0)
-        round_y(2, 1, False)
-        decode(2, 9, 1, 0)
-        encode(("z", 2, 4), 1)
+        skip(0, 3, 0)
         quantize(("z", 2, 1))
-        skip(1, 5, 1)
-        turn_y(("y", 0, 1), 1)
-        add_bias(5, 1)
-        interleave(("z", 2, 4), 0, 256, True)
-        decode(2, 8, 0, 1)
-        copy_words(("y", 0, 1), 1, False)
-        decode(2, 8, 0, 2)
-        decode(2, 8, 0, 3)
-        finish(5, 1)
+        decode(1, 7, 1, 0)
+        quantize(("z", 2, 2))
+        encode(("z", 2, 5), 2)
+        decode(1, 7, 1, 1)
+        skip_last(2, 0)
+        decode(2, 9, 0, 0)
         decode(2, 9, 0, 1)
+        skip_last(1, 0)
         decode(2, 9, 0, 2)
-        quantize_y(("y", 0, 1))
+        store_y(2, 0)
+        decode(1, 7, 1, 2)
+        interleave(("z", 2, 3), 0, 256, "A")
+        skip_last(6, 0)
+        decode(1, 7, 1, 3)
+        store_y(1, 0)
+        decode(2, 8, 0, 0)
+        skip_last(4, 0)
+        decode(2, 8, 0, 1)
+        store_y(6, 0)
+        decode(2, 8, 0, 2)
+        decode(1, 7, 1, 4)
+        skip_last(3, 0)
+        interleave(("z", 2, 4), 0, 256, "A")
+        store_y(4, 0)
+        decode(1, 7, 1, 5)
+        skip(1, 5, 0)
+        quantize(("z", 2, 3))
+        store_y(3, 0)
+        skip(1, 7, 0)
+        round_y(6, 0, "V")
+        decode(1, 5, 1, 0)
+        skip_last(5, 0)
+        interleave(("z", 2, 5), 0, 256, "A")
         decode(2, 9, 0, 3)
-        store_y(5, 1)
-        round_y(5, 1, True)
-        decode(2, 8, 1, 1)
-        decode(2, 8, 1, 2)
+        decode(2, 8, 0, 3)
         quantize(("z", 2, 4))
-        store_words(("y", 0, 1))
-        decode(2, 8, 1, 3)
-        decode(2, 8, 0, 4)
-        decode(2, 8, 0, 5)
+        decode(1, 5, 1, 1)
+        store_y(5, 0)
+        round_y(5, 0, "V")
+        decode(1, 5, 1, 2)
         decode(2, 9, 0, 4)
+        skip_last(7, 0)
+        interleave(("s", 1, 0), 0, 512, "A")
+        decode(2, 8, 0, 4)
+        decode(1, 5, 1, 3)
+        quantize(("z", 2, 5))
+        store_y(7, 0)
+        decode(1, 5, 1, 4)
+        round_y(7, 0, "V")
+        decode(1, 5, 1, 5)
+        round_y(4, 0, "V")
         decode(2, 9, 0, 5)
-        finish(8, 0)
-        decode(2, 8, 1, 4)
-        decode(2, 8, 1, 5)
-        finish(9, 0)
-        store_y(8, 0)
-        round_y(8, 0, True)
+        round_y(3, 0, "V")
+        decode(2, 8, 0, 5)
+        turn_y(("y", 1, 0), 0)
+        bias_first(9, 0)
+        turn_y(("y", 1, 0), 1)
+        bias_first(8, 0)
+        round_y(1, 0, "A")
+        decode(2, 9, 1, 0)
+        skip(2, 9, 0)
+        quantize(("s", 1, 0))
+        copy_words(("y", 1, 0), 0, "A")
+        skip(2, 8, 0)
         decode(2, 9, 1, 1)
+        skip_last(9, 0)
+        copy_words(("y", 1, 0), 1, "A")
         decode(2, 9, 1, 2)
-        finish(8, 1)
+        skip(1, 4, 1)
+        skip_last(8, 0)
+        round_y(0, 0, "A")
+        skip(1, 6, 1)
         store_y(9, 0)
+        skip(1, 5, 1)
+        add_bias(4, 1)
+        round_y(9, 0, "A")
+        skip(1, 7, 1)
+        store_y(8, 0)
+        skip(2, 9, 1)
+        add_bias(6, 1)
         decode(2, 9, 1, 3)
-        round_y(9, 0, True)
+        round_y(8, 0, "A")
+        skip(2, 8, 1)
+        add_bias(5, 1)
         decode(2, 9, 1, 4)
-        store_y(8, 1)
-        decode(2, 9, 1, 5)
-        turn_y(("y", 1, 1), 0)
-        finish(9, 1)
+        round_y(2, 0, "A")
+        turn_y(("y", 0, 0), 0)
+        add_bias(7, 1)
         turn_y(("y", 2, 0), 0)
-        copy_words(("y", 1, 1), 0, True)
-        round_y(8, 1, False)
-        store_y(9, 1)
-        round_y(9, 1, False)
-        copy_words(("y", 2, 0), 0, True)
-        quantize_y(("y", 1, 1))
-        turn_y(("y", 2, 1), 0)
+        copy_words(("y", 0, 0), 0, "A")
+        decode(2, 9, 1, 5)
+        finish(5, 1)
+        turn_y(("y", 0, 0), 1)
+        copy_words(("y", 2, 0), 0, "A")
+        finish(7, 1)
+        store_y(5, 1)
+        skip(0, 3, 1)
+        round_y(5, 1, "A")
+        add_bias(9, 1)
+        skip(0, 1, 1)
+        store_y(7, 1)
+        skip(0, 0, 1)
+        copy_words(("y", 0, 0), 1, "A")
+        add_bias(8, 1)
+        skip(0, 2, 1)
+        decode(1, 6, 1, 0)
+        round_y(7, 1, "A")
+        quantize_y(("y", 1, 0))
+        decode(1, 6, 1, 1)
+        decode(1, 6, 1, 2)
+        decode(1, 6, 1, 3)
         quantize_y(("y", 2, 0))
-        copy_words(("y", 2, 1), 0, True)
-        store_words(("y", 1, 1))
+        store_words(("y", 1, 0))
+        decode(1, 6, 1, 4)
+        skip_last(3, 1)
         store_words(("y", 2, 0))
+        decode(1, 6, 1, 5)
+        decode(1, 4, 1, 0)
+        skip_last(1, 1)
+        decode(1, 4, 1, 1)
+        store_y(3, 1)
+        round_y(3, 1, "A")
+        decode(1, 4, 1, 2)
+        finish(6, 1)
+        decode(1, 4, 1, 3)
+        store_y(1, 1)
+        round_y(1, 1, "A")
+        decode(1, 4, 1, 4)
+        skip_last(0, 1)
+        decode(1, 4, 1, 5)
+        store_y(6, 1)
+        round_y(6, 1, "A")
+        decode(2, 8, 1, 0)
+        skip_last(2, 1)
+        decode(2, 8, 1, 1)
+        store_y(0, 1)
+        round_y(0, 1, "A")
+        decode(2, 8, 1, 2)
+        finish(4, 1)
+        turn_y(("y", 1, 1), 1)
+        store_y(2, 1)
+        decode(2, 8, 1, 3)
+        quantize_y(("y", 0, 0))
+        store_y(4, 1)
+        copy_words(("y", 1, 1), 1, "A")
+        decode(2, 8, 1, 4)
+        round_y(4, 1, "V")
+        decode(2, 8, 1, 5)
         store_scales(0)
+        round_y(2, 1, "A")
+        turn_y(("y", 0, 1), 0)
+        finish(9, 1)
+        store_words(("y", 0, 0))
+        turn_y(("y", 1, 1), 0)
+        finish(8, 1)
+        copy_words(("y", 0, 1), 0, "A")
+        turn_y(("y", 0, 1), 1)
+        store_y(9, 1)
+        round_y(9, 1, "V")
+        copy_words(("y", 1, 1), 0, "A")
+        store_y(8, 1)
+        round_y(8, 1, "V")
+        copy_words(("y", 0, 1), 1, "A")
+        turn_y(("y", 2, 1), 0)
+        quantize_y(("y", 1, 1))
+        copy_words(("y", 2, 1), 0, "A")
+        quantize_y(("y", 0, 1))
+        store_words(("y", 1, 1))
         quantize_y(("y", 2, 1))
+        store_words(("y", 0, 1))
         store_words(("y", 2, 1))
         store_scales(1)

@@ -35,9 +35,9 @@ def tile_sae_relu_decode_skip_g1_kernel(tc, pre, b_enc, g, w_dec, b_dec, r, x, w
         ident = keep.tile([P, P], F32, name="ident")
         ident_bf = keep.tile([P, P], BF16, name="ident_bf")
         vec_rows = keep.tile([P, KP], BF16, name="vec_rows")
-        sign = keep.tile([P, G, PACK], F32, name="sign")
-        g_abs = keep.tile([P, G, PACK], F32, name="g_abs")
-        gb = keep.tile([P, G, PACK], F32, name="gb")
+        half_sign = keep.tile([P, 2, 2 * G], F32, name="half_sign")
+        g_abs = keep.tile([P, 2, 2 * G], F32, name="g_abs")
+        gb = keep.tile([P, 2, 2 * G], F32, name="gb")
         r_col = keep.tile([P, M // P], F32, name="r_col")
         b_all = keep.tile([P, D], BF16, name="b_all")
         y_codes = [keep.tile([P, M], U32, name="y_codes%d" % n, align_bytes=64) for n in range(2)]
@@ -66,29 +66,47 @@ def tile_sae_relu_decode_skip_g1_kernel(tc, pre, b_enc, g, w_dec, b_dec, r, x, w
             else:
                 nc.gpsimd.tensor_scalar(out=dst, in0=src, scalar1=1.0, scalar2=-0.0, op0=ALU.mult, op1=ALU.add)
 
-        def constants_load():
+        def constants_zero():
             nc.vector.memset(vec_rows[:].bitcast(U32), 0)
+
+        def identity():
             make_identity(nc, ident[:])
+
+        def identity_bf():
+            nc.scalar.copy(out=ident_bf[:], in_=ident[:])
+
+        def constants_load():
             for vec, row in ((g, 0), (b_enc, B_ROW)):
                 rows = vec.rearrange("(c k) -> c k", k=KP)
                 nc.sync.dma_start(out=vec_rows[row:row + 4, :], in_=rows[0:4])
                 nc.sync.dma_start(out=vec_rows[row + 4:row + G, :], in_=rows[4:G])
-            nc.scalar.copy(out=ident_bf[:], in_=ident[:])
+
+        def load_half(u, h):
+            if u not in raw:
+                raw[u] = work.tile([P, 2, PACK, HALF // 2], BF16, name="raw", bufs=10)
+            cols = slice(h * HALF // 2, (h + 1) * HALF // 2)
+            nc.sync.dma_start(out=raw[u][:, h], in_=w_skip[:, cols].rearrange("(p j) d -> p j d", j=PACK))
 
         def constants_turn():
             bank = take("vec", [P, 2, P], F32)
             for h in range(2):
                 nc.tensor.transpose(bank[:, h, :], vec_rows[:].bitcast(F32)[:, h::2], ident[:])
 
+        def vec_cols(row):
+            vals = banks["vec"][:].rearrange("p h c -> p (h c)").bitcast(BF16).rearrange("p (h v) -> p h v", h=2)
+            return vals[:, :, 2 * row:2 * (row + G)]
+
+        def sign_make():
+            nc.vector.tensor_scalar(out=half_sign[:], in0=vec_cols(0), scalar1=0.0, scalar2=-0.5, op0=ALU.is_ge, op1=ALU.add)
+
         def constants_make():
-            vals = banks["vec"][:].rearrange("p h c -> p (h c)").bitcast(BF16).rearrange("p (h c e) -> p c h e", h=2, e=2)
-            g_t, b_t = vals[:, 0:G], vals[:, B_ROW:B_ROW + G]
-            split = lambda t: t[:].rearrange("p c (h e) -> p c h e", e=2)
-            nc.vector.tensor_scalar(out=split(sign), in0=g_t, scalar1=0.0, scalar2=2.0, op0=ALU.is_ge, op1=ALU.mult)
-            nc.vector.tensor_scalar(out=sign[:], in0=sign[:], scalar1=-1.0, scalar2=None, op0=ALU.add)
-            nc.vector.tensor_tensor(out=split(g_abs), in0=g_t, in1=split(sign), op=ALU.mult)
-            nc.vector.tensor_tensor(out=split(gb), in0=b_t, in1=split(g_abs), op=ALU.mult)
+            nc.vector.scalar_tensor_tensor(out=g_abs[:], in0=vec_cols(0), scalar=2.0, in1=half_sign[:], op0=ALU.mult, op1=ALU.mult)
+            nc.vector.tensor_tensor(out=gb[:], in0=vec_cols(B_ROW), in1=g_abs[:], op=ALU.mult)
             release("vec")
+
+        def per_k(t, k, j):
+            col = 2 * k + j % 2
+            return t[:, j // 2, col:col + 1]
 
         def r_load():
             rows = r.rearrange("(m p) o -> m (p o)", p=P)
@@ -134,13 +152,13 @@ def tile_sae_relu_decode_skip_g1_kernel(tc, pre, b_enc, g, w_dec, b_dec, r, x, w
                 for e in range(2):
                     j = 2 * hh + e
                     nc.scalar.activation(out=slots[u][:, j, 0:w], in_=banks[u, h][:, i, :].bitcast(BF16)[:, e::2], func=ACT.Relu,
-                                         bias=gb[:, u[2], j:j + 1], scale=g_abs[:, u[2], j:j + 1])
+                                         bias=per_k(gb, u[2], j), scale=per_k(g_abs, u[2], j))
             release((u, h))
 
         def sign_w(u):
             for j in range(PACK):
-                nc.vector.tensor_scalar(out=raw[u][:, j, :], in0=raw[u][:, j, :], scalar1=sign[:, u[2], j:j + 1],
-                                        scalar2=None, op0=ALU.mult)
+                nc.vector.tensor_scalar(out=raw[u][:, j, :], in0=raw[u][:, j, :], scalar1=per_k(half_sign, u[2], j),
+                                        scalar2=2.0, op0=ALU.mult, op1=ALU.mult)
 
         def new_grouped(u):
             if u not in grouped:
@@ -148,7 +166,12 @@ def tile_sae_relu_decode_skip_g1_kernel(tc, pre, b_enc, g, w_dec, b_dec, r, x, w
             return grouped[u]
 
         def interleave(u, c0, c1, engine):
-            src = slots.get(u, raw[u])[:, :, c0:c1].rearrange("p t (c i) -> p c t i", i=4)
+            if u == ("s", 0, 0):
+                h = c0 // (HALF // 2)
+                rows = raw[u][:, h, :, c0 - h * HALF // 2:c1 - h * HALF // 2]
+            else:
+                rows = slots.get(u, raw[u])[:, :, c0:c1]
+            src = rows.rearrange("p t (c i) -> p c t i", i=4)
             dst = new_grouped(u)[:, c0 * PACK:c1 * PACK].rearrange("p (c i t) -> p c t i", i=4, t=PACK)
             move(engine, dst, src)
 
@@ -234,469 +257,476 @@ def tile_sae_relu_decode_skip_g1_kernel(tc, pre, b_enc, g, w_dec, b_dec, r, x, w
             dst = out_1[u[2]].rearrange("p m t -> p (m t)").bitcast(I32)
             nc.sync.dma_start(out=dst[:, token_cols(u)], in_=y_codes[u[2]][:, token_cols(u)].bitcast(I32))
 
-        def store_scales(n):
-            for q in range(4):
-                eng = nc.scalar if q % 2 else nc.sync
+        def store_scales(n, h):
+            eng = nc.scalar if n and h else nc.sync
+            for q in range(2 * h, 2 * h + 2):
                 eng.dma_start(out=out_2[n, 4 * q:4 * q + 4, :].bitcast(I32),
                               in_=y_scales[n][32 * q:32 * q + 4, :].bitcast(I32))
 
-        load(("s", 0, 0))
+        load_half(("s", 0, 0), 1)
+        identity()
+        identity_bf()
+        constants_zero()
         constants_load()
-        load(("x", 0, 0))
-        load(("w", 0, 1))
-        load(("w", 0, 0))
-        load(("w", 0, 2))
-        load(("z", 0, 0))
-        load(("w", 0, 3))
-        load(("z", 0, 1))
-        load(("z", 0, 2))
-        interleave(("s", 0, 0), 0, 256, "V")
-        interleave(("s", 0, 0), 256, 512, "A")
         constants_turn()
+        sign_make()
         constants_make()
-        load(("x", 2, 0))
-        turn_x(("x", 0, 0), 0)
+        interleave(("s", 0, 0), 424, 512, "A")
+        interleave(("s", 0, 0), 256, 424, "V")
+        load(("z", 0, 3))
+        load_half(("s", 0, 0), 0)
+        turn_z(("z", 0, 3), 1)
+        interleave(("s", 0, 0), 168, 256, "A")
+        interleave(("s", 0, 0), 0, 168, "V")
+        load(("w", 0, 0))
         quantize(("s", 0, 0))
+        load(("z", 0, 0))
+        sign_w(("w", 0, 0))
+        interleave(("w", 0, 0), 160, 512, "V")
+        encode(("z", 0, 3), 1)
+        turn_z(("z", 0, 3), 0)
+        encode(("z", 0, 3), 0)
+        interleave(("z", 0, 3), 160, 512, "V")
+        load(("w", 0, 4))
+        interleave(("w", 0, 0), 0, 160, "A")
+        turn_z(("z", 0, 0), 1)
+        turn_z(("z", 0, 0), 0)
+        sign_w(("w", 0, 4))
+        quantize(("w", 0, 0))
+        interleave(("z", 0, 3), 0, 160, "A")
+        load(("z", 0, 4))
+        encode(("z", 0, 0), 0)
+        encode(("z", 0, 0), 1)
+        turn_z(("z", 0, 4), 1)
+        load(("z", 0, 1))
+        load(("z", 1, 2))
+        quantize(("z", 0, 3))
+        interleave(("w", 0, 4), 0, 512, "V")
+        interleave(("z", 0, 0), 0, 512, "V")
+        turn_z(("z", 0, 4), 0)
+        encode(("z", 0, 4), 1)
+        r_load()
+        quantize(("w", 0, 4))
+        turn_z(("z", 0, 1), 0)
+        quantize(("z", 0, 0))
+        turn_z(("z", 1, 2), 0)
+        turn_z(("z", 0, 1), 1)
+        turn_z(("z", 1, 2), 1)
+        r_turn()
+        decode(0, 1, 0, 0)
+        load(("w", 0, 1))
+        load(("z", 0, 2))
+        encode(("z", 0, 4), 0)
+        sign_w(("w", 0, 1))
+        load(("z", 0, 5))
+        encode(("z", 1, 2), 0)
+        encode(("z", 0, 1), 0)
+        interleave(("z", 0, 4), 0, 512, "V")
+        encode(("z", 0, 1), 1)
+        interleave(("w", 0, 1), 0, 512, "V")
+        turn_z(("z", 0, 2), 0)
+        load(("w", 0, 2))
+        interleave(("z", 0, 1), 0, 512, "V")
+        encode(("z", 1, 2), 1)
+        turn_z(("z", 0, 5), 1)
+        quantize(("w", 0, 1))
+        quantize(("z", 0, 1))
+        sign_w(("w", 0, 2))
+        turn_z(("z", 0, 2), 1)
+        turn_z(("z", 0, 5), 0)
+        load(("x", 1, 0))
+        load(("z", 1, 3))
+        encode(("z", 0, 2), 1)
+        encode(("z", 0, 5), 0)
+        turn_z(("z", 1, 3), 0)
+        turn_x(("x", 1, 0), 1)
+        load(("x", 0, 0))
+        load(("z", 1, 1))
+        turn_x(("x", 1, 0), 0)
+        load(("w", 0, 3))
+        load(("z", 1, 0))
+        interleave(("z", 1, 2), 0, 512, "V")
+        turn_x(("x", 0, 0), 0)
+        load(("z", 1, 5))
+        load(("w", 0, 5))
+        interleave(("w", 0, 2), 0, 512, "V")
+        r_copy()
+        encode(("z", 0, 2), 0)
+        encode(("z", 0, 5), 1)
+        encode(("z", 1, 3), 0)
+        quantize(("z", 0, 4))
+        interleave(("z", 0, 5), 0, 512, "V")
+        load(("z", 1, 4))
+        turn_z(("z", 1, 3), 1)
+        decode(0, 0, 0, 0)
+        turn_z(("z", 1, 1), 1)
+        copy_words(("x", 1, 0), 1, "A")
+        copy_words(("x", 1, 0), 0, "A")
+        quantize(("w", 0, 2))
+        turn_z(("z", 1, 1), 0)
+        turn_z(("z", 1, 0), 0)
+        decode(0, 2, 0, 0)
+        encode(("z", 1, 1), 1)
+        interleave(("z", 0, 2), 0, 512, "V")
         turn_x(("x", 0, 0), 1)
         copy_words(("x", 0, 0), 0, "A")
-        sign_w(("w", 0, 1))
-        load(("w", 0, 4))
-        copy_words(("x", 0, 0), 1, "A")
-        quantize(("x", 0, 0))
-        interleave(("w", 0, 1), 0, 256, "A")
-        load(("z", 1, 1))
-        sign_w(("w", 0, 0))
-        interleave(("w", 0, 1), 256, 512, "V")
-        interleave(("w", 0, 0), 0, 512, "A")
-        r_load()
-        sign_w(("w", 0, 2))
-        quantize(("w", 0, 1))
-        interleave(("w", 0, 2), 0, 512, "V")
-        load(("z", 1, 0))
-        turn_z(("z", 0, 0), 0)
-        turn_z(("z", 0, 0), 1)
-        encode(("z", 0, 0), 0)
-        quantize(("w", 0, 0))
-        load(("w", 0, 5))
-        quantize(("w", 0, 2))
-        encode(("z", 0, 0), 1)
-        sign_w(("w", 0, 3))
-        load(("z", 0, 3))
-        turn_z(("z", 0, 1), 0)
-        turn_z(("z", 0, 1), 1)
-        interleave(("z", 0, 0), 0, 256, "V")
-        interleave(("z", 0, 0), 256, 512, "A")
-        interleave(("w", 0, 3), 0, 512, "V")
-        load(("z", 1, 2))
-        turn_z(("z", 0, 2), 0)
-        turn_z(("z", 0, 2), 1)
-        encode(("z", 0, 1), 0)
-        load(("z", 1, 3))
-        turn_x(("x", 2, 0), 0)
-        quantize(("z", 0, 0))
-        encode(("z", 0, 1), 1)
-        quantize(("w", 0, 3))
-        load(("z", 0, 4))
         decode(0, 3, 0, 0)
-        sign_w(("w", 0, 4))
-        decode(0, 0, 0, 0)
-        decode(0, 2, 0, 0)
-        encode(("z", 0, 2), 0)
-        decode(0, 1, 0, 0)
-        interleave(("z", 0, 1), 0, 512, "V")
-        load(("z", 0, 5))
-        turn_z(("z", 1, 1), 0)
-        load(("z", 1, 5))
-        encode(("z", 0, 2), 1)
-        r_turn()
-        interleave(("w", 0, 4), 0, 256, "V")
-        bias_load()
-        quantize(("z", 0, 1))
-        r_copy()
-        encode(("z", 1, 1), 0)
-        turn_z(("z", 1, 1), 1)
-        interleave(("z", 0, 2), 0, 256, "V")
         decode(0, 3, 0, 1)
-        load(("x", 1, 0))
-        decode(0, 0, 0, 1)
-        sign_w(("w", 0, 5))
-        encode(("z", 1, 1), 1)
-        decode(0, 2, 0, 1)
-        decode(0, 1, 0, 1)
-        interleave(("z", 0, 2), 256, 512, "V")
-        turn_z(("z", 1, 0), 0)
-        copy_words(("x", 2, 0), 0, "A")
-        interleave(("w", 0, 4), 256, 512, "V")
-        turn_z(("z", 1, 0), 1)
-        encode(("z", 1, 0), 0)
-        turn_z(("z", 0, 3), 0)
-        quantize(("z", 0, 2))
-        load(("w", 1, 0))
-        turn_z(("z", 0, 3), 1)
-        load(("z", 1, 4))
-        quantize(("x", 2, 0))
-        quantize(("w", 0, 4))
-        encode(("z", 1, 0), 1)
-        decode(0, 3, 0, 2)
-        decode(0, 0, 0, 2)
-        interleave(("z", 1, 1), 0, 512, "V")
-        decode(0, 2, 0, 2)
-        load(("w", 1, 1))
-        decode(0, 1, 0, 2)
-        encode(("z", 0, 3), 0)
-        turn_z(("z", 1, 2), 0)
-        interleave(("z", 1, 0), 0, 256, "V")
-        turn_z(("z", 1, 2), 1)
-        encode(("z", 0, 3), 1)
-        quantize(("z", 1, 1))
-        turn_z(("z", 1, 3), 0)
-        load(("w", 1, 2))
-        interleave(("z", 1, 0), 256, 512, "V")
-        encode(("z", 1, 2), 0)
-        turn_z(("z", 1, 3), 1)
-        interleave(("w", 0, 5), 0, 256, "V")
-        quantize(("z", 1, 0))
-        load(("w", 1, 3))
-        encode(("z", 1, 2), 1)
-        turn_z(("z", 0, 4), 0)
-        interleave(("w", 0, 5), 256, 512, "V")
-        interleave(("z", 0, 3), 0, 256, "V")
-        encode(("z", 1, 3), 0)
-        load(("w", 1, 4))
-        turn_z(("z", 0, 4), 1)
-        quantize(("w", 0, 5))
-        load(("w", 1, 5))
-        interleave(("z", 0, 3), 256, 512, "V")
+        encode(("z", 1, 1), 0)
         encode(("z", 1, 3), 1)
-        turn_z(("z", 0, 5), 0)
-        interleave(("z", 1, 2), 0, 256, "V")
-        encode(("z", 0, 4), 0)
-        quantize(("z", 0, 3))
-        turn_z(("z", 0, 5), 1)
-        interleave(("z", 1, 2), 256, 512, "V")
-        decode(0, 3, 0, 3)
+        decode(0, 0, 0, 1)
         load(("z", 2, 0))
-        encode(("z", 0, 4), 1)
-        decode(0, 0, 0, 3)
-        sign_w(("w", 1, 0))
-        decode(0, 2, 0, 3)
-        decode(0, 1, 0, 3)
-        quantize(("z", 1, 2))
-        decode(1, 5, 0, 0)
-        encode(("z", 0, 5), 0)
-        decode(1, 5, 0, 1)
-        interleave(("z", 1, 3), 0, 512, "V")
-        turn_z(("z", 1, 5), 0)
-        decode(1, 5, 0, 2)
-        encode(("z", 0, 5), 1)
-        turn_z(("z", 1, 5), 1)
-        interleave(("z", 0, 4), 0, 256, "V")
-        quantize(("z", 1, 3))
-        load(("z", 2, 1))
-        encode(("z", 1, 5), 0)
-        turn_z(("z", 1, 4), 0)
-        sign_w(("w", 1, 1))
-        decode(1, 5, 0, 3)
-        encode(("z", 1, 5), 1)
-        sign_w(("w", 1, 2))
-        turn_z(("z", 1, 4), 1)
-        interleave(("z", 0, 4), 256, 512, "V")
-        load(("z", 2, 2))
-        interleave(("z", 0, 5), 0, 256, "A")
-        sign_w(("w", 1, 3))
-        turn_x(("x", 1, 0), 0)
-        quantize(("z", 0, 4))
-        encode(("z", 1, 4), 0)
-        sign_w(("w", 1, 4))
-        decode(0, 3, 0, 4)
-        decode(0, 0, 0, 4)
-        interleave(("z", 0, 5), 256, 512, "V")
-        decode(0, 2, 0, 4)
-        encode(("z", 1, 4), 1)
-        decode(0, 1, 0, 4)
-        sign_w(("w", 1, 5))
-        turn_x(("x", 1, 0), 1)
-        copy_words(("x", 1, 0), 0, "A")
+        copy_words(("x", 0, 0), 1, "A")
         quantize(("z", 0, 5))
-        turn_z(("z", 2, 0), 2)
-        load(("z", 2, 3))
-        copy_words(("x", 1, 0), 1, "A")
-        interleave(("z", 1, 5), 0, 512, "V")
-        turn_z(("z", 2, 1), 2)
-        load(("z", 2, 4))
-        encode(("z", 2, 0), 2)
-        decode(0, 3, 0, 5)
+        sign_w(("w", 0, 3))
+        quantize(("z", 0, 2))
+        interleave(("w", 0, 3), 0, 512, "V")
+        sign_w(("w", 0, 5))
+        turn_z(("z", 1, 0), 1)
+        decode(0, 1, 0, 1)
+        load(("w", 1, 0))
         load(("z", 2, 5))
-        decode(0, 0, 0, 5)
+        turn_z(("z", 1, 4), 1)
+        quantize(("w", 0, 3))
+        load(("w", 1, 5))
+        load(("w", 1, 1))
+        load(("x", 2, 0))
+        quantize(("x", 0, 0))
+        interleave(("w", 0, 5), 480, 512, "V")
         quantize(("x", 1, 0))
-        decode(0, 2, 0, 5)
+        encode(("z", 1, 0), 0)
+        encode(("z", 1, 0), 1)
+        interleave(("z", 1, 1), 0, 512, "V")
+        interleave(("z", 1, 0), 0, 512, "V")
+        decode(0, 2, 0, 1)
+        turn_z(("z", 1, 5), 1)
+        turn_z(("z", 1, 5), 0)
+        interleave(("w", 0, 5), 0, 480, "A")
+        decode(0, 1, 0, 2)
+        quantize(("w", 0, 5))
+        sign_w(("w", 1, 1))
+        turn_z(("z", 1, 4), 0)
+        decode(0, 0, 0, 2)
+        decode(0, 3, 0, 2)
+        decode(0, 0, 0, 3)
+        decode(0, 2, 0, 2)
+        load(("z", 2, 3))
+        bias_load()
+        encode(("z", 1, 4), 0)
+        encode(("z", 1, 5), 0)
+        quantize(("z", 1, 1))
+        encode(("z", 1, 5), 1)
+        encode(("z", 1, 4), 1)
+        decode(0, 0, 0, 4)
+        decode(0, 2, 0, 3)
+        interleave(("z", 1, 3), 0, 512, "A")
+        decode(0, 1, 0, 3)
+        decode(0, 2, 0, 4)
+        interleave(("z", 1, 4), 0, 512, "A")
+        quantize(("z", 1, 0))
+        quantize(("z", 1, 2))
+        interleave(("z", 1, 5), 0, 192, "A")
+        decode(0, 3, 0, 3)
+        decode(0, 3, 0, 4)
+        decode(0, 3, 0, 5)
+        sign_w(("w", 1, 0))
+        decode(0, 1, 0, 4)
+        decode(0, 0, 0, 5)
         decode(0, 1, 0, 5)
-        encode(("z", 2, 1), 2)
-        bias_first(0, 0)
-        decode(1, 6, 0, 0)
-        decode(1, 6, 0, 1)
-        decode(1, 6, 0, 2)
-        bias_first(1, 0)
-        decode(1, 6, 0, 3)
-        decode(1, 7, 0, 0)
-        bias_first(2, 0)
-        interleave(("w", 1, 0), 0, 512, "A")
-        decode(1, 7, 0, 1)
-        decode(1, 7, 0, 2)
         bias_first(3, 0)
-        decode(1, 7, 0, 3)
-        decode(1, 4, 0, 0)
-        quantize(("z", 1, 5))
-        decode(1, 4, 0, 1)
-        decode(1, 4, 0, 2)
-        interleave(("z", 1, 4), 0, 512, "V")
-        decode(1, 4, 0, 3)
-        skip(0, 0, 0)
-        turn_z(("z", 2, 2), 2)
-        interleave(("w", 1, 1), 0, 256, "A")
-        load(("s", 1, 0))
-        quantize(("w", 1, 0))
-        turn_z(("z", 2, 3), 2)
-        turn_z(("z", 2, 4), 2)
-        quantize(("z", 1, 4))
-        encode(("z", 2, 2), 2)
-        interleave(("w", 1, 1), 256, 512, "V")
-        decode(1, 5, 0, 4)
-        decode(1, 5, 0, 5)
-        interleave(("w", 1, 2), 0, 256, "V")
-        interleave(("w", 1, 2), 256, 512, "A")
-        decode(1, 6, 0, 4)
-        decode(1, 6, 0, 5)
-        bias_first(5, 0)
-        decode(0, 3, 1, 0)
-        decode(1, 7, 0, 4)
-        bias_first(6, 0)
-        decode(1, 7, 0, 5)
-        interleave(("w", 1, 3), 0, 512, "A")
-        decode(0, 2, 1, 0)
-        quantize(("w", 1, 1))
-        decode(1, 4, 0, 4)
-        decode(1, 4, 0, 5)
-        bias_first(7, 0)
-        decode(0, 1, 1, 0)
-        decode(0, 3, 1, 1)
-        decode(0, 2, 1, 1)
-        bias_first(4, 0)
-        decode(0, 1, 1, 1)
-        decode(0, 0, 1, 0)
-        quantize(("w", 1, 2))
-        decode(0, 0, 1, 1)
-        interleave(("w", 1, 4), 0, 256, "A")
-        turn_z(("z", 2, 5), 2)
-        quantize(("w", 1, 3))
-        decode(0, 3, 1, 2)
-        interleave(("w", 1, 4), 256, 512, "V")
-        decode(0, 3, 1, 3)
-        interleave(("w", 1, 5), 0, 256, "A")
-        decode(0, 2, 1, 2)
-        interleave(("w", 1, 5), 256, 512, "V")
-        decode(0, 2, 1, 3)
-        decode(0, 1, 1, 2)
-        quantize(("w", 1, 4))
-        decode(0, 1, 1, 3)
-        interleave(("z", 2, 0), 0, 256, "A")
-        decode(0, 0, 1, 2)
-        quantize(("w", 1, 5))
-        decode(0, 0, 1, 3)
-        decode(0, 3, 1, 4)
-        skip_last(0, 0)
-        decode(0, 2, 1, 4)
-        decode(0, 3, 1, 5)
-        interleave(("z", 2, 1), 0, 256, "A")
-        decode(0, 2, 1, 5)
-        interleave(("z", 2, 2), 0, 256, "V")
-        store_y(0, 0)
-        decode(0, 1, 1, 4)
-        decode(0, 1, 1, 5)
-        bias_first(2, 1)
-        decode(0, 0, 1, 4)
-        encode(("z", 2, 3), 2)
-        decode(0, 0, 1, 5)
-        bias_first(1, 1)
-        skip(0, 2, 0)
+        decode(0, 2, 0, 5)
+        bias_first(2, 0)
+        bias_first(1, 0)
+        decode(1, 6, 0, 0)
+        decode(1, 5, 0, 0)
+        decode(1, 5, 0, 1)
+        decode(1, 6, 0, 1)
         skip(0, 1, 0)
-        bias_first(0, 1)
-        bias_first(3, 1)
-        encode(("z", 2, 4), 2)
-        skip(1, 6, 0)
-        skip(1, 4, 0)
-        quantize(("z", 2, 0))
-        skip(0, 3, 0)
-        quantize(("z", 2, 1))
-        decode(1, 7, 1, 0)
-        quantize(("z", 2, 2))
-        encode(("z", 2, 5), 2)
-        decode(1, 7, 1, 1)
+        skip(0, 2, 0)
+        decode(1, 5, 0, 2)
+        decode(1, 6, 0, 2)
+        decode(1, 7, 0, 0)
+        interleave(("w", 1, 0), 0, 288, "A")
         skip_last(2, 0)
-        decode(2, 9, 0, 0)
-        decode(2, 9, 0, 1)
+        bias_first(0, 0)
+        skip(0, 3, 0)
+        load(("w", 1, 2))
+        load(("w", 1, 4))
         skip_last(1, 0)
-        decode(2, 9, 0, 2)
-        store_y(2, 0)
-        decode(1, 7, 1, 2)
-        interleave(("z", 2, 3), 0, 256, "A")
-        skip_last(6, 0)
-        decode(1, 7, 1, 3)
-        store_y(1, 0)
-        decode(2, 8, 0, 0)
-        skip_last(4, 0)
-        decode(2, 8, 0, 1)
-        store_y(6, 0)
-        decode(2, 8, 0, 2)
-        decode(1, 7, 1, 4)
+        decode(1, 4, 0, 0)
+        decode(1, 7, 0, 1)
+        decode(1, 4, 0, 1)
         skip_last(3, 0)
-        interleave(("z", 2, 4), 0, 256, "A")
-        store_y(4, 0)
-        decode(1, 7, 1, 5)
-        skip(1, 5, 0)
-        quantize(("z", 2, 3))
-        store_y(3, 0)
-        skip(1, 7, 0)
-        round_y(6, 0, "V")
-        decode(1, 5, 1, 0)
-        skip_last(5, 0)
-        interleave(("z", 2, 5), 0, 256, "A")
-        decode(2, 9, 0, 3)
-        decode(2, 8, 0, 3)
-        quantize(("z", 2, 4))
-        decode(1, 5, 1, 1)
-        store_y(5, 0)
-        round_y(5, 0, "V")
-        decode(1, 5, 1, 2)
-        decode(2, 9, 0, 4)
-        skip_last(7, 0)
-        interleave(("s", 1, 0), 0, 512, "A")
-        decode(2, 8, 0, 4)
-        decode(1, 5, 1, 3)
-        quantize(("z", 2, 5))
-        store_y(7, 0)
-        decode(1, 5, 1, 4)
-        round_y(7, 0, "V")
-        decode(1, 5, 1, 5)
-        round_y(4, 0, "V")
-        decode(2, 9, 0, 5)
-        round_y(3, 0, "V")
-        decode(2, 8, 0, 5)
-        turn_y(("y", 1, 0), 0)
-        bias_first(9, 0)
-        turn_y(("y", 1, 0), 1)
-        bias_first(8, 0)
-        round_y(1, 0, "A")
-        decode(2, 9, 1, 0)
-        skip(2, 9, 0)
-        quantize(("s", 1, 0))
-        copy_words(("y", 1, 0), 0, "A")
-        skip(2, 8, 0)
-        decode(2, 9, 1, 1)
-        skip_last(9, 0)
-        copy_words(("y", 1, 0), 1, "A")
-        decode(2, 9, 1, 2)
-        skip(1, 4, 1)
-        skip_last(8, 0)
-        round_y(0, 0, "A")
-        skip(1, 6, 1)
-        store_y(9, 0)
-        skip(1, 5, 1)
-        add_bias(4, 1)
-        round_y(9, 0, "A")
-        skip(1, 7, 1)
-        store_y(8, 0)
-        skip(2, 9, 1)
-        add_bias(6, 1)
-        decode(2, 9, 1, 3)
-        round_y(8, 0, "A")
-        skip(2, 8, 1)
-        add_bias(5, 1)
-        decode(2, 9, 1, 4)
-        round_y(2, 0, "A")
-        turn_y(("y", 0, 0), 0)
-        add_bias(7, 1)
-        turn_y(("y", 2, 0), 0)
-        copy_words(("y", 0, 0), 0, "A")
-        decode(2, 9, 1, 5)
-        finish(5, 1)
-        turn_y(("y", 0, 0), 1)
-        copy_words(("y", 2, 0), 0, "A")
-        finish(7, 1)
-        store_y(5, 1)
-        skip(0, 3, 1)
-        round_y(5, 1, "A")
-        add_bias(9, 1)
-        skip(0, 1, 1)
-        store_y(7, 1)
-        skip(0, 0, 1)
-        copy_words(("y", 0, 0), 1, "A")
-        add_bias(8, 1)
-        skip(0, 2, 1)
+        skip(0, 0, 0)
+        load(("z", 2, 1))
+        turn_z(("z", 2, 0), 2)
+        turn_z(("z", 2, 1), 2)
+        skip_last(0, 0)
+        quantize(("z", 1, 3))
+        turn_x(("x", 2, 0), 0)
+        turn_z(("z", 2, 5), 2)
+        interleave(("z", 1, 5), 192, 512, "V")
+        load(("z", 2, 2))
+        decode(1, 7, 0, 2)
+        interleave(("w", 1, 1), 0, 512, "G")
+        quantize(("z", 1, 4))
+        decode(1, 5, 0, 3)
+        interleave(("w", 1, 0), 288, 512, "G")
+        store_y(1, 0)
+        load(("w", 1, 3))
+        decode(1, 7, 0, 3)
+        decode(1, 4, 0, 2)
+        decode(1, 4, 0, 3)
+        quantize(("z", 1, 5))
+        quantize(("w", 1, 1))
+        load(("z", 2, 4))
+        copy_words(("x", 2, 0), 0, "A")
+        encode(("z", 2, 1), 2)
+        decode(1, 6, 0, 3)
+        decode(1, 6, 0, 4)
+        store_y(2, 0)
+        quantize(("w", 1, 0))
+        decode(1, 7, 0, 4)
+        sign_w(("w", 1, 2))
+        interleave(("w", 1, 2), 224, 512, "G")
+        sign_w(("w", 1, 3))
+        decode(1, 4, 0, 4)
+        decode(1, 5, 0, 4)
+        decode(1, 7, 0, 5)
+        bias_first(7, 0)
+        encode(("z", 2, 5), 2)
+        interleave(("w", 1, 2), 0, 224, "A")
+        decode(1, 4, 0, 5)
+        load(("s", 1, 0))
+        interleave(("w", 1, 3), 0, 448, "A")
+        decode(0, 3, 1, 0)
+        decode(0, 3, 1, 1)
+        decode(1, 6, 0, 5)
+        bias_first(6, 0)
+        decode(0, 0, 1, 0)
+        decode(1, 5, 0, 5)
+        bias_first(5, 0)
+        decode(0, 0, 1, 1)
+        interleave(("w", 1, 3), 448, 512, "G")
+        bias_first(4, 0)
+        skip(1, 6, 0)
+        decode(0, 2, 1, 0)
+        decode(0, 1, 1, 0)
+        decode(0, 1, 1, 1)
+        decode(0, 2, 1, 1)
+        skip_last(6, 0)
+        quantize(("w", 1, 2))
         decode(1, 6, 1, 0)
-        round_y(7, 1, "A")
-        quantize_y(("y", 1, 0))
+        decode(1, 5, 1, 0)
+        sign_w(("w", 1, 4))
+        interleave(("w", 1, 4), 448, 512, "G")
         decode(1, 6, 1, 1)
+        decode(1, 5, 1, 1)
+        skip(1, 7, 0)
         decode(1, 6, 1, 2)
+        encode(("z", 2, 0), 2)
+        decode(0, 1, 1, 2)
+        decode(1, 5, 1, 2)
+        interleave(("w", 1, 4), 0, 160, "A")
+        decode(0, 3, 1, 2)
+        decode(0, 0, 1, 2)
+        interleave(("z", 2, 0), 0, 256, "A")
+        decode(0, 2, 1, 2)
+        quantize(("w", 1, 3))
+        skip_last(7, 0)
+        interleave(("w", 1, 4), 160, 448, "V")
+        decode(0, 2, 1, 3)
         decode(1, 6, 1, 3)
-        quantize_y(("y", 2, 0))
-        store_words(("y", 1, 0))
-        decode(1, 6, 1, 4)
-        skip_last(3, 1)
-        store_words(("y", 2, 0))
-        decode(1, 6, 1, 5)
         decode(1, 4, 1, 0)
-        skip_last(1, 1)
+        decode(0, 0, 1, 3)
+        sign_w(("w", 1, 5))
+        interleave(("w", 1, 5), 0, 128, "A")
+        round_y(0, 0, "A")
+        decode(0, 3, 1, 3)
+        round_y(7, 0, "A")
+        interleave(("z", 2, 5), 0, 256, "A")
+        decode(1, 5, 1, 3)
+        decode(0, 1, 1, 3)
+        quantize(("w", 1, 4))
+        interleave(("w", 1, 5), 128, 512, "V")
+        interleave(("z", 2, 1), 0, 256, "A")
+        skip(1, 5, 0)
+        quantize(("x", 2, 0))
+        interleave(("s", 1, 0), 96, 512, "G")
+        round_y(1, 0, "A")
+        interleave(("s", 1, 0), 0, 96, "A")
+        round_y(3, 0, "G")
         decode(1, 4, 1, 1)
-        store_y(3, 1)
-        round_y(3, 1, "A")
+        round_y(6, 0, "G")
+        quantize(("w", 1, 5))
+        skip_last(5, 0)
         decode(1, 4, 1, 2)
-        finish(6, 1)
+        decode(0, 3, 1, 4)
+        decode(0, 1, 1, 4)
         decode(1, 4, 1, 3)
-        store_y(1, 1)
-        round_y(1, 1, "A")
+        decode(1, 5, 1, 4)
+        decode(0, 2, 1, 4)
+        decode(1, 6, 1, 4)
+        decode(0, 3, 1, 5)
+        bias_first(3, 1)
+        decode(0, 0, 1, 4)
+        decode(0, 1, 1, 5)
         decode(1, 4, 1, 4)
-        skip_last(0, 1)
+        round_y(2, 0, "A")
+        decode(0, 0, 1, 5)
+        decode(1, 6, 1, 5)
+        decode(1, 5, 1, 5)
+        bias_first(1, 1)
+        bias_first(0, 1)
         decode(1, 4, 1, 5)
-        store_y(6, 1)
-        round_y(6, 1, "A")
-        decode(2, 8, 1, 0)
-        skip_last(2, 1)
-        decode(2, 8, 1, 1)
+        decode(0, 2, 1, 5)
+        skip(1, 4, 0)
+        bias_first(5, 1)
+        bias_first(2, 1)
+        bias_first(6, 1)
+        store_y(6, 0)
+        store_y(5, 0)
+        turn_z(("z", 2, 2), 2)
+        encode(("z", 2, 2), 2)
+        turn_y(("y", 0, 0), 0)
+        turn_z(("z", 2, 4), 2)
+        turn_y(("y", 0, 0), 1)
+        turn_y(("y", 1, 0), 1)
+        quantize(("z", 2, 0))
+        quantize(("s", 1, 0))
+        skip_last(4, 0)
+        bias_first(4, 1)
+        store_y(4, 0)
+        store_y(3, 0)
+        copy_words(("y", 0, 0), 0, "A")
+        turn_z(("z", 2, 3), 2)
+        skip(0, 0, 1)
+        decode(1, 7, 1, 0)
+        decode(1, 7, 1, 1)
+        copy_words(("y", 1, 0), 1, "A")
+        encode(("z", 2, 3), 2)
+        decode(1, 7, 1, 2)
+        decode(1, 7, 1, 3)
+        skip(1, 7, 1)
+        skip(2, 9, 0)
+        skip_last(0, 1)
+        quantize(("z", 2, 1))
+        skip(0, 1, 1)
+        decode(1, 7, 1, 4)
+        decode(1, 7, 1, 5)
+        interleave(("z", 2, 2), 0, 256, "G")
+        quantize(("z", 2, 2))
+        add_bias(7, 1)
+        add_bias(9, 0)
+        interleave(("z", 2, 3), 192, 256, "G")
+        encode(("z", 2, 4), 2)
+        finish(7, 1)
+        interleave(("z", 2, 4), 0, 256, "G")
+        skip(1, 5, 1)
+        decode(2, 8, 0, 0)
+        copy_words(("y", 0, 0), 1, "A")
+        decode(2, 9, 0, 0)
+        skip(0, 2, 1)
+        interleave(("z", 2, 3), 0, 192, "A")
+        decode(2, 9, 0, 1)
+        skip(0, 3, 1)
+        decode(2, 9, 0, 2)
         store_y(0, 1)
-        round_y(0, 1, "A")
-        decode(2, 8, 1, 2)
-        finish(4, 1)
-        turn_y(("y", 1, 1), 1)
+        store_y(7, 1)
+        skip_last(5, 1)
+        skip_last(1, 1)
+        store_y(0, 0)
+        skip(2, 9, 1)
+        decode(2, 8, 0, 1)
+        skip(1, 4, 1)
+        skip(1, 6, 1)
+        store_y(1, 1)
+        skip_last(2, 1)
+        decode(2, 8, 0, 2)
+        decode(2, 9, 1, 0)
+        round_y(5, 0, "A")
+        quantize(("z", 2, 3))
+        quantize(("z", 2, 5))
+        skip_last(3, 1)
         store_y(2, 1)
-        decode(2, 8, 1, 3)
-        quantize_y(("y", 0, 0))
-        store_y(4, 1)
-        copy_words(("y", 1, 1), 1, "A")
-        decode(2, 8, 1, 4)
-        round_y(4, 1, "V")
-        decode(2, 8, 1, 5)
-        store_scales(0)
+        decode(2, 9, 0, 3)
+        skip(2, 8, 0)
+        quantize(("z", 2, 4))
+        store_y(3, 1)
+        round_y(4, 0, "A")
         round_y(2, 1, "A")
-        turn_y(("y", 0, 1), 0)
-        finish(9, 1)
-        store_words(("y", 0, 0))
-        turn_y(("y", 1, 1), 0)
-        finish(8, 1)
-        copy_words(("y", 0, 1), 0, "A")
+        add_bias(9, 1)
+        decode(2, 9, 1, 1)
+        decode(2, 8, 0, 3)
+        decode(2, 8, 0, 4)
+        decode(2, 8, 0, 5)
+        decode(2, 9, 1, 2)
+        decode(2, 9, 1, 3)
+        round_y(0, 1, "A")
+        add_bias(8, 0)
+        round_y(3, 1, "A")
+        round_y(1, 1, "A")
+        store_y(5, 1)
+        store_y(7, 0)
+        turn_y(("y", 1, 0), 0)
+        quantize_y(("y", 0, 0))
+        finish(8, 0)
+        store_y(8, 0)
         turn_y(("y", 0, 1), 1)
-        store_y(9, 1)
+        skip_last(4, 1)
+        store_y(4, 1)
+        store_words(("y", 0, 0))
+        round_y(7, 1, "G")
+        skip_last(6, 1)
+        turn_y(("y", 0, 1), 0)
+        decode(2, 9, 0, 4)
+        copy_words(("y", 1, 0), 0, "A")
+        decode(2, 9, 0, 5)
+        finish(9, 0)
+        decode(2, 8, 1, 0)
+        decode(2, 8, 1, 1)
+        store_y(9, 0)
+        copy_words(("y", 0, 1), 0, "A")
+        round_y(4, 1, "G")
+        quantize_y(("y", 1, 0))
+        store_words(("y", 1, 0))
+        decode(2, 8, 1, 2)
+        skip(2, 8, 1)
+        store_y(6, 1)
+        round_y(8, 0, "A")
+        round_y(5, 1, "A")
+        round_y(9, 0, "A")
+        add_bias(8, 1)
+        decode(2, 9, 1, 4)
+        decode(2, 9, 1, 5)
+        finish(9, 1)
+        decode(2, 8, 1, 3)
+        decode(2, 8, 1, 4)
+        decode(2, 8, 1, 5)
+        copy_words(("y", 0, 1), 1, "A")
+        round_y(6, 1, "A")
+        finish(8, 1)
+        turn_y(("y", 2, 0), 0)
         round_y(9, 1, "V")
+        store_y(9, 1)
+        copy_words(("y", 2, 0), 0, "A")
+        turn_y(("y", 1, 1), 0)
         copy_words(("y", 1, 1), 0, "A")
         store_y(8, 1)
         round_y(8, 1, "V")
-        copy_words(("y", 0, 1), 1, "A")
-        turn_y(("y", 2, 1), 0)
-        quantize_y(("y", 1, 1))
-        copy_words(("y", 2, 1), 0, "A")
+        quantize_y(("y", 2, 0))
         quantize_y(("y", 0, 1))
-        store_words(("y", 1, 1))
-        quantize_y(("y", 2, 1))
+        turn_y(("y", 1, 1), 1)
+        store_scales(0, 0)
+        store_scales(0, 1)
+        store_words(("y", 2, 0))
         store_words(("y", 0, 1))
+        copy_words(("y", 1, 1), 1, "A")
+        quantize_y(("y", 1, 1))
+        store_words(("y", 1, 1))
+        turn_y(("y", 2, 1), 0)
+        copy_words(("y", 2, 1), 0, "A")
+        quantize_y(("y", 2, 1))
         store_words(("y", 2, 1))
-        store_scales(1)
+        store_scales(1, 1)
+        store_scales(1, 0)

@@ -171,8 +171,9 @@ def tile_sae_relu_decode_skip_g1_kernel(tc, pre, b_enc, g, w_dec, b_dec, r, x, w
                 rows = raw[u][:, h, :, c0 - h * HALF // 2:c1 - h * HALF // 2]
             else:
                 rows = slots.get(u, raw[u])[:, :, c0:c1]
-            src = rows.rearrange("p t (c i) -> p c t i", i=4)
-            dst = new_grouped(u)[:, c0 * PACK:c1 * PACK].rearrange("p (c i t) -> p c t i", i=4, t=PACK)
+            run = 1 if engine == "G" else 4
+            src = rows.rearrange("p t (c i) -> p c t i", i=run)
+            dst = new_grouped(u)[:, c0 * PACK:c1 * PACK].rearrange("p (c i t) -> p c t i", i=run, t=PACK)
             move(engine, dst, src)
 
         def quantize(u):
@@ -263,470 +264,468 @@ def tile_sae_relu_decode_skip_g1_kernel(tc, pre, b_enc, g, w_dec, b_dec, r, x, w
                 eng.dma_start(out=out_2[n, 4 * q:4 * q + 4, :].bitcast(I32),
                               in_=y_scales[n][32 * q:32 * q + 4, :].bitcast(I32))
 
-        load_half(("s", 0, 0), 1)
         identity()
-        identity_bf()
         constants_zero()
+        load(("z", 0, 0))
         constants_load()
+        load(("w", 0, 0))
+        load(("z", 0, 2))
+        load(("z", 0, 4))
+        identity_bf()
         constants_turn()
+        turn_z(("z", 0, 0), 1)
+        load(("w", 0, 2))
+        turn_z(("z", 0, 0), 0)
+        turn_z(("z", 0, 2), 1)
         sign_make()
         constants_make()
-        interleave(("s", 0, 0), 424, 512, "A")
-        interleave(("s", 0, 0), 256, 424, "V")
-        load(("z", 0, 3))
-        load_half(("s", 0, 0), 0)
-        turn_z(("z", 0, 3), 1)
-        interleave(("s", 0, 0), 168, 256, "A")
-        interleave(("s", 0, 0), 0, 168, "V")
-        load(("w", 0, 0))
-        quantize(("s", 0, 0))
-        load(("z", 0, 0))
-        sign_w(("w", 0, 0))
-        interleave(("w", 0, 0), 160, 512, "V")
-        encode(("z", 0, 3), 1)
-        turn_z(("z", 0, 3), 0)
-        encode(("z", 0, 3), 0)
-        interleave(("z", 0, 3), 160, 512, "V")
-        load(("w", 0, 4))
-        interleave(("w", 0, 0), 0, 160, "A")
-        turn_z(("z", 0, 0), 1)
-        turn_z(("z", 0, 0), 0)
-        sign_w(("w", 0, 4))
-        quantize(("w", 0, 0))
-        interleave(("z", 0, 3), 0, 160, "A")
-        load(("z", 0, 4))
-        encode(("z", 0, 0), 0)
-        encode(("z", 0, 0), 1)
-        turn_z(("z", 0, 4), 1)
-        load(("z", 0, 1))
-        load(("z", 1, 2))
-        quantize(("z", 0, 3))
-        interleave(("w", 0, 4), 0, 512, "V")
-        interleave(("z", 0, 0), 0, 512, "V")
-        turn_z(("z", 0, 4), 0)
-        encode(("z", 0, 4), 1)
-        r_load()
-        quantize(("w", 0, 4))
-        turn_z(("z", 0, 1), 0)
-        quantize(("z", 0, 0))
-        turn_z(("z", 1, 2), 0)
-        turn_z(("z", 0, 1), 1)
-        turn_z(("z", 1, 2), 1)
-        r_turn()
-        decode(0, 1, 0, 0)
-        load(("w", 0, 1))
-        load(("z", 0, 2))
-        encode(("z", 0, 4), 0)
-        sign_w(("w", 0, 1))
-        load(("z", 0, 5))
-        encode(("z", 1, 2), 0)
-        encode(("z", 0, 1), 0)
-        interleave(("z", 0, 4), 0, 512, "V")
-        encode(("z", 0, 1), 1)
-        interleave(("w", 0, 1), 0, 512, "V")
         turn_z(("z", 0, 2), 0)
-        load(("w", 0, 2))
-        interleave(("z", 0, 1), 0, 512, "V")
-        encode(("z", 1, 2), 1)
-        turn_z(("z", 0, 5), 1)
-        quantize(("w", 0, 1))
-        quantize(("z", 0, 1))
-        sign_w(("w", 0, 2))
-        turn_z(("z", 0, 2), 1)
-        turn_z(("z", 0, 5), 0)
-        load(("x", 1, 0))
-        load(("z", 1, 3))
+        load(("z", 0, 1))
+        encode(("z", 0, 0), 1)
+        load(("w", 0, 1))
+        turn_z(("z", 0, 4), 0)
+        load(("z", 0, 5))
+        load(("z", 0, 3))
+        turn_z(("z", 0, 4), 1)
+        sign_w(("w", 0, 0))
+        interleave(("w", 0, 0), 0, 512, "V")
+        quantize(("w", 0, 0))
+        encode(("z", 0, 0), 0)
+        interleave(("z", 0, 0), 0, 512, "V")
+        turn_z(("z", 0, 1), 0)
         encode(("z", 0, 2), 1)
-        encode(("z", 0, 5), 0)
-        turn_z(("z", 1, 3), 0)
-        turn_x(("x", 1, 0), 1)
+        sign_w(("w", 0, 2))
+        turn_z(("z", 0, 1), 1)
+        quantize(("z", 0, 0))
+        encode(("z", 0, 4), 0)
+        encode(("z", 0, 4), 1)
+        encode(("z", 0, 2), 0)
         load(("x", 0, 0))
-        load(("z", 1, 1))
-        turn_x(("x", 1, 0), 0)
+        interleave(("w", 0, 2), 0, 512, "V")
+        interleave(("z", 0, 4), 0, 512, "V")
+        encode(("z", 0, 1), 0)
+        encode(("z", 0, 1), 1)
+        interleave(("z", 0, 2), 0, 192, "A")
+        sign_w(("w", 0, 1))
+        interleave(("z", 0, 2), 192, 512, "V")
         load(("w", 0, 3))
         load(("z", 1, 0))
-        interleave(("z", 1, 2), 0, 512, "V")
-        turn_x(("x", 0, 0), 0)
-        load(("z", 1, 5))
-        load(("w", 0, 5))
-        interleave(("w", 0, 2), 0, 512, "V")
-        r_copy()
-        encode(("z", 0, 2), 0)
+        load(("z", 1, 2))
+        load(("z", 1, 1))
+        turn_z(("z", 0, 5), 1)
+        turn_z(("z", 0, 3), 1)
+        turn_z(("z", 0, 3), 0)
+        turn_z(("z", 0, 5), 0)
+        decode(0, 1, 0, 0)
         encode(("z", 0, 5), 1)
-        encode(("z", 1, 3), 0)
+        encode(("z", 0, 5), 0)
+        interleave(("w", 0, 1), 0, 512, "V")
+        turn_x(("x", 0, 0), 0)
+        encode(("z", 0, 3), 1)
         quantize(("z", 0, 4))
-        interleave(("z", 0, 5), 0, 512, "V")
-        load(("z", 1, 4))
-        turn_z(("z", 1, 3), 1)
-        decode(0, 0, 0, 0)
-        turn_z(("z", 1, 1), 1)
-        copy_words(("x", 1, 0), 1, "A")
-        copy_words(("x", 1, 0), 0, "A")
-        quantize(("w", 0, 2))
-        turn_z(("z", 1, 1), 0)
-        turn_z(("z", 1, 0), 0)
-        decode(0, 2, 0, 0)
-        encode(("z", 1, 1), 1)
-        interleave(("z", 0, 2), 0, 512, "V")
-        turn_x(("x", 0, 0), 1)
-        copy_words(("x", 0, 0), 0, "A")
-        decode(0, 3, 0, 0)
-        decode(0, 3, 0, 1)
-        encode(("z", 1, 1), 0)
-        encode(("z", 1, 3), 1)
-        decode(0, 0, 0, 1)
-        load(("z", 2, 0))
-        copy_words(("x", 0, 0), 1, "A")
-        quantize(("z", 0, 5))
+        interleave(("z", 0, 1), 0, 512, "V")
+        load(("w", 0, 5))
+        load(("z", 1, 3))
         sign_w(("w", 0, 3))
-        quantize(("z", 0, 2))
-        interleave(("w", 0, 3), 0, 512, "V")
-        sign_w(("w", 0, 5))
+        quantize(("w", 0, 2))
+        decode(0, 3, 0, 0)
+        turn_x(("x", 0, 0), 1)
+        quantize(("z", 0, 1))
         turn_z(("z", 1, 0), 1)
-        decode(0, 1, 0, 1)
-        load(("w", 1, 0))
-        load(("z", 2, 5))
-        turn_z(("z", 1, 4), 1)
-        quantize(("w", 0, 3))
-        load(("w", 1, 5))
-        load(("w", 1, 1))
-        load(("x", 2, 0))
-        quantize(("x", 0, 0))
-        interleave(("w", 0, 5), 480, 512, "V")
-        quantize(("x", 1, 0))
-        encode(("z", 1, 0), 0)
+        turn_z(("z", 1, 0), 0)
+        turn_z(("z", 1, 1), 0)
+        encode(("z", 0, 3), 0)
         encode(("z", 1, 0), 1)
-        interleave(("z", 1, 1), 0, 512, "V")
+        load(("w", 1, 0))
+        encode(("z", 1, 0), 0)
+        copy_words(("x", 0, 0), 1, "A")
+        r_load()
+        load(("w", 0, 4))
+        interleave(("z", 0, 5), 0, 512, "V")
+        interleave(("z", 0, 3), 0, 512, "V")
+        quantize(("w", 0, 1))
+        quantize(("z", 0, 5))
+        encode(("z", 1, 1), 0)
+        turn_z(("z", 1, 2), 1)
+        load(("x", 2, 0))
+        turn_z(("z", 1, 1), 1)
         interleave(("z", 1, 0), 0, 512, "V")
+        interleave(("w", 0, 3), 160, 512, "V")
+        sign_w(("w", 0, 5))
+        quantize(("z", 1, 0))
+        decode(0, 0, 0, 0)
+        encode(("z", 1, 1), 1)
+        decode(0, 0, 0, 1)
+        decode(0, 3, 0, 1)
+        load(("z", 1, 4))
+        turn_z(("z", 1, 2), 0)
+        turn_z(("z", 1, 3), 1)
+        decode(0, 1, 0, 1)
+        interleave(("w", 0, 3), 0, 160, "A")
+        encode(("z", 1, 2), 1)
+        copy_words(("x", 0, 0), 0, "A")
+        turn_z(("z", 1, 3), 0)
+        encode(("z", 1, 3), 1)
+        turn_x(("x", 2, 0), 0)
+        copy_words(("x", 2, 0), 0, "A")
+        turn_z(("z", 1, 4), 1)
+        decode(0, 2, 0, 0)
         decode(0, 2, 0, 1)
-        turn_z(("z", 1, 5), 1)
-        turn_z(("z", 1, 5), 0)
-        interleave(("w", 0, 5), 0, 480, "A")
-        decode(0, 1, 0, 2)
-        quantize(("w", 0, 5))
-        sign_w(("w", 1, 1))
-        turn_z(("z", 1, 4), 0)
+        r_turn()
+        load(("z", 1, 5))
+        quantize(("z", 0, 2))
+        encode(("z", 1, 2), 0)
+        quantize(("w", 0, 3))
+        load(("z", 2, 2))
         decode(0, 0, 0, 2)
+        decode(0, 1, 0, 2)
+        sign_w(("w", 0, 4))
+        interleave(("z", 1, 1), 0, 512, "V")
+        interleave(("w", 0, 5), 256, 512, "V")
+        quantize(("z", 0, 3))
+        quantize(("z", 1, 1))
+        interleave(("w", 0, 4), 0, 512, "V")
+        r_copy()
+        encode(("z", 1, 3), 0)
+        decode(0, 2, 0, 2)
+        interleave(("z", 1, 2), 0, 512, "V")
+        encode(("z", 1, 4), 1)
+        interleave(("w", 0, 5), 0, 256, "A")
+        decode(1, 5, 0, 0)
         decode(0, 3, 0, 2)
         decode(0, 0, 0, 3)
-        decode(0, 2, 0, 2)
-        load(("z", 2, 3))
-        bias_load()
-        encode(("z", 1, 4), 0)
-        encode(("z", 1, 5), 0)
-        quantize(("z", 1, 1))
-        encode(("z", 1, 5), 1)
-        encode(("z", 1, 4), 1)
-        decode(0, 0, 0, 4)
-        decode(0, 2, 0, 3)
-        interleave(("z", 1, 3), 0, 512, "A")
-        decode(0, 1, 0, 3)
-        decode(0, 2, 0, 4)
-        interleave(("z", 1, 4), 0, 512, "A")
-        quantize(("z", 1, 0))
-        quantize(("z", 1, 2))
-        interleave(("z", 1, 5), 0, 192, "A")
+        decode(1, 5, 0, 1)
+        quantize(("w", 0, 4))
         decode(0, 3, 0, 3)
+        turn_z(("z", 1, 4), 0)
+        load(("z", 2, 3))
+        load_half(("s", 0, 0), 0)
+        load(("z", 2, 1))
+        turn_z(("z", 1, 5), 0)
+        encode(("z", 1, 4), 0)
+        load(("x", 1, 0))
+        load_half(("s", 0, 0), 1)
+        turn_z(("z", 1, 5), 1)
+        decode(0, 2, 0, 3)
         decode(0, 3, 0, 4)
-        decode(0, 3, 0, 5)
+        decode(0, 1, 0, 3)
+        quantize(("w", 0, 5))
         sign_w(("w", 1, 0))
+        quantize(("x", 0, 0))
+        bias_load()
+        interleave(("w", 1, 0), 0, 512, "V")
+        load(("w", 1, 3))
+        turn_x(("x", 1, 0), 1)
         decode(0, 1, 0, 4)
-        decode(0, 0, 0, 5)
         decode(0, 1, 0, 5)
-        bias_first(3, 0)
+        decode(0, 3, 0, 5)
+        decode(0, 2, 0, 4)
+        quantize(("x", 2, 0))
+        load(("z", 2, 0))
+        encode(("z", 1, 5), 0)
+        encode(("z", 1, 5), 1)
+        quantize(("w", 1, 0))
+        quantize(("z", 1, 2))
+        copy_words(("x", 1, 0), 1, "A")
+        load(("s", 1, 0))
+        interleave(("z", 1, 3), 0, 512, "A")
         decode(0, 2, 0, 5)
+        decode(0, 0, 0, 4)
+        decode(0, 0, 0, 5)
+        bias_first(0, 0)
         bias_first(2, 0)
         bias_first(1, 0)
+        bias_first(3, 0)
+        load(("w", 1, 1))
         decode(1, 6, 0, 0)
-        decode(1, 5, 0, 0)
-        decode(1, 5, 0, 1)
         decode(1, 6, 0, 1)
-        skip(0, 1, 0)
-        skip(0, 2, 0)
-        decode(1, 5, 0, 2)
+        turn_z(("z", 2, 3), 2)
+        quantize(("z", 1, 3))
+        interleave(("s", 0, 0), 256, 424, "V")
+        sign_w(("w", 1, 1))
+        interleave(("z", 1, 4), 192, 512, "G")
+        interleave(("z", 1, 5), 0, 352, "A")
+        interleave(("s", 0, 0), 424, 512, "A")
+        turn_z(("z", 2, 2), 2)
+        turn_x(("x", 1, 0), 0)
+        interleave(("z", 1, 4), 0, 192, "A")
+        copy_words(("x", 1, 0), 0, "A")
+        interleave(("s", 0, 0), 168, 256, "A")
+        load(("w", 1, 2))
+        sign_w(("w", 1, 3))
+        load(("w", 1, 5))
+        decode(1, 4, 0, 0)
         decode(1, 6, 0, 2)
         decode(1, 7, 0, 0)
-        interleave(("w", 1, 0), 0, 288, "A")
-        skip_last(2, 0)
-        bias_first(0, 0)
-        skip(0, 3, 0)
-        load(("w", 1, 2))
-        load(("w", 1, 4))
-        skip_last(1, 0)
-        decode(1, 4, 0, 0)
+        decode(1, 5, 0, 2)
         decode(1, 7, 0, 1)
-        decode(1, 4, 0, 1)
-        skip_last(3, 0)
-        skip(0, 0, 0)
-        load(("z", 2, 1))
-        turn_z(("z", 2, 0), 2)
-        turn_z(("z", 2, 1), 2)
-        skip_last(0, 0)
-        quantize(("z", 1, 3))
-        turn_x(("x", 2, 0), 0)
-        turn_z(("z", 2, 5), 2)
-        interleave(("z", 1, 5), 192, 512, "V")
-        load(("z", 2, 2))
         decode(1, 7, 0, 2)
-        interleave(("w", 1, 1), 0, 512, "G")
-        quantize(("z", 1, 4))
-        decode(1, 5, 0, 3)
-        interleave(("w", 1, 0), 288, 512, "G")
-        store_y(1, 0)
-        load(("w", 1, 3))
         decode(1, 7, 0, 3)
+        interleave(("z", 1, 5), 352, 512, "V")
+        quantize(("z", 1, 4))
+        interleave(("s", 0, 0), 0, 168, "V")
+        interleave(("w", 1, 1), 0, 512, "A")
+        quantize(("z", 1, 5))
+        decode(1, 5, 0, 3)
+        decode(1, 4, 0, 1)
         decode(1, 4, 0, 2)
         decode(1, 4, 0, 3)
-        quantize(("z", 1, 5))
-        quantize(("w", 1, 1))
-        load(("z", 2, 4))
-        copy_words(("x", 2, 0), 0, "A")
-        encode(("z", 2, 1), 2)
-        decode(1, 6, 0, 3)
-        decode(1, 6, 0, 4)
-        store_y(2, 0)
-        quantize(("w", 1, 0))
-        decode(1, 7, 0, 4)
+        turn_z(("z", 2, 0), 2)
+        turn_z(("z", 2, 1), 2)
+        quantize(("s", 0, 0))
         sign_w(("w", 1, 2))
-        interleave(("w", 1, 2), 224, 512, "G")
-        sign_w(("w", 1, 3))
-        decode(1, 4, 0, 4)
+        quantize(("w", 1, 1))
         decode(1, 5, 0, 4)
-        decode(1, 7, 0, 5)
-        bias_first(7, 0)
-        encode(("z", 2, 5), 2)
-        interleave(("w", 1, 2), 0, 224, "A")
-        decode(1, 4, 0, 5)
-        load(("s", 1, 0))
-        interleave(("w", 1, 3), 0, 448, "A")
-        decode(0, 3, 1, 0)
-        decode(0, 3, 1, 1)
+        encode(("z", 2, 1), 2)
+        decode(1, 7, 0, 4)
+        decode(1, 6, 0, 3)
+        decode(1, 5, 0, 5)
+        decode(1, 6, 0, 4)
         decode(1, 6, 0, 5)
         bias_first(6, 0)
-        decode(0, 0, 1, 0)
-        decode(1, 5, 0, 5)
-        bias_first(5, 0)
-        decode(0, 0, 1, 1)
-        interleave(("w", 1, 3), 448, 512, "G")
+        decode(1, 7, 0, 5)
+        decode(1, 4, 0, 4)
+        decode(1, 4, 0, 5)
         bias_first(4, 0)
-        skip(1, 6, 0)
+        encode(("z", 2, 3), 2)
+        decode(1, 6, 1, 0)
+        decode(1, 6, 1, 1)
+        bias_first(5, 0)
+        bias_first(7, 0)
+        decode(0, 3, 1, 0)
+        decode(0, 3, 1, 1)
+        encode(("z", 2, 0), 2)
+        skip(0, 1, 0)
+        decode(1, 5, 1, 0)
+        skip(0, 0, 0)
+        decode(1, 5, 1, 1)
+        skip_last(1, 0)
+        interleave(("w", 1, 2), 128, 512, "G")
+        skip(0, 2, 0)
+        decode(1, 4, 1, 0)
+        load(("w", 1, 4))
+        load(("z", 2, 4))
+        skip_last(0, 0)
+        load(("z", 2, 5))
+        skip_last(2, 0)
+        skip(0, 3, 0)
+        decode(1, 4, 1, 1)
+        decode(0, 0, 1, 0)
+        decode(0, 0, 1, 1)
         decode(0, 2, 1, 0)
+        interleave(("w", 1, 2), 0, 128, "A")
+        interleave(("w", 1, 3), 0, 416, "A")
+        quantize(("w", 1, 2))
+        decode(0, 2, 1, 1)
+        decode(0, 3, 1, 2)
+        sign_w(("w", 1, 4))
+        decode(0, 2, 1, 2)
+        decode(1, 4, 1, 2)
+        skip_last(3, 0)
+        interleave(("w", 1, 3), 416, 512, "G")
+        quantize(("w", 1, 3))
+        decode(0, 0, 1, 2)
+        interleave(("w", 1, 4), 0, 512, "A")
+        sign_w(("w", 1, 5))
+        skip(2, 8, 0)
+        decode(1, 5, 1, 2)
+        decode(1, 6, 1, 2)
+        decode(1, 5, 1, 3)
+        add_bias(8, 0)
+        decode(0, 0, 1, 3)
+        decode(0, 3, 1, 3)
+        interleave(("w", 1, 5), 0, 288, "A")
+        interleave(("w", 1, 5), 288, 512, "V")
+        interleave(("s", 1, 0), 0, 224, "A")
+        interleave(("z", 2, 0), 0, 256, "A")
+        quantize(("w", 1, 4))
+        decode(0, 2, 1, 3)
         decode(0, 1, 1, 0)
         decode(0, 1, 1, 1)
-        decode(0, 2, 1, 1)
-        skip_last(6, 0)
-        quantize(("w", 1, 2))
-        decode(1, 6, 1, 0)
-        decode(1, 5, 1, 0)
-        sign_w(("w", 1, 4))
-        interleave(("w", 1, 4), 448, 512, "G")
-        decode(1, 6, 1, 1)
-        decode(1, 5, 1, 1)
-        skip(1, 7, 0)
-        decode(1, 6, 1, 2)
-        encode(("z", 2, 0), 2)
+        interleave(("s", 1, 0), 224, 512, "V")
         decode(0, 1, 1, 2)
-        decode(1, 5, 1, 2)
-        interleave(("w", 1, 4), 0, 160, "A")
-        decode(0, 3, 1, 2)
-        decode(0, 0, 1, 2)
-        interleave(("z", 2, 0), 0, 256, "A")
-        decode(0, 2, 1, 2)
-        quantize(("w", 1, 3))
-        skip_last(7, 0)
-        interleave(("w", 1, 4), 160, 448, "V")
-        decode(0, 2, 1, 3)
-        decode(1, 6, 1, 3)
-        decode(1, 4, 1, 0)
-        decode(0, 0, 1, 3)
-        sign_w(("w", 1, 5))
-        interleave(("w", 1, 5), 0, 128, "A")
-        round_y(0, 0, "A")
-        decode(0, 3, 1, 3)
-        round_y(7, 0, "A")
-        interleave(("z", 2, 5), 0, 256, "A")
-        decode(1, 5, 1, 3)
-        decode(0, 1, 1, 3)
-        quantize(("w", 1, 4))
-        interleave(("w", 1, 5), 128, 512, "V")
-        interleave(("z", 2, 1), 0, 256, "A")
-        skip(1, 5, 0)
-        quantize(("x", 2, 0))
-        interleave(("s", 1, 0), 96, 512, "G")
-        round_y(1, 0, "A")
-        interleave(("s", 1, 0), 0, 96, "A")
-        round_y(3, 0, "G")
-        decode(1, 4, 1, 1)
-        round_y(6, 0, "G")
-        quantize(("w", 1, 5))
-        skip_last(5, 0)
-        decode(1, 4, 1, 2)
-        decode(0, 3, 1, 4)
-        decode(0, 1, 1, 4)
         decode(1, 4, 1, 3)
+        decode(0, 1, 1, 3)
         decode(1, 5, 1, 4)
+        quantize(("w", 1, 5))
+        quantize(("x", 1, 0))
         decode(0, 2, 1, 4)
-        decode(1, 6, 1, 4)
-        decode(0, 3, 1, 5)
-        bias_first(3, 1)
-        decode(0, 0, 1, 4)
-        decode(0, 1, 1, 5)
-        decode(1, 4, 1, 4)
-        round_y(2, 0, "A")
-        decode(0, 0, 1, 5)
-        decode(1, 6, 1, 5)
-        decode(1, 5, 1, 5)
-        bias_first(1, 1)
-        bias_first(0, 1)
-        decode(1, 4, 1, 5)
-        decode(0, 2, 1, 5)
-        skip(1, 4, 0)
-        bias_first(5, 1)
-        bias_first(2, 1)
-        bias_first(6, 1)
-        store_y(6, 0)
-        store_y(5, 0)
-        turn_z(("z", 2, 2), 2)
-        encode(("z", 2, 2), 2)
-        turn_y(("y", 0, 0), 0)
-        turn_z(("z", 2, 4), 2)
-        turn_y(("y", 0, 0), 1)
-        turn_y(("y", 1, 0), 1)
-        quantize(("z", 2, 0))
         quantize(("s", 1, 0))
-        skip_last(4, 0)
-        bias_first(4, 1)
-        store_y(4, 0)
+        decode(0, 3, 1, 4)
+        decode(1, 6, 1, 3)
+        decode(1, 6, 1, 4)
+        decode(0, 2, 1, 5)
+        decode(1, 5, 1, 5)
         store_y(3, 0)
-        copy_words(("y", 0, 0), 0, "A")
-        turn_z(("z", 2, 3), 2)
-        skip(0, 0, 1)
-        decode(1, 7, 1, 0)
-        decode(1, 7, 1, 1)
-        copy_words(("y", 1, 0), 1, "A")
-        encode(("z", 2, 3), 2)
-        decode(1, 7, 1, 2)
-        decode(1, 7, 1, 3)
-        skip(1, 7, 1)
-        skip(2, 9, 0)
-        skip_last(0, 1)
-        quantize(("z", 2, 1))
-        skip(0, 1, 1)
-        decode(1, 7, 1, 4)
-        decode(1, 7, 1, 5)
-        interleave(("z", 2, 2), 0, 256, "G")
-        quantize(("z", 2, 2))
-        add_bias(7, 1)
-        add_bias(9, 0)
-        interleave(("z", 2, 3), 192, 256, "G")
-        encode(("z", 2, 4), 2)
-        finish(7, 1)
-        interleave(("z", 2, 4), 0, 256, "G")
-        skip(1, 5, 1)
-        decode(2, 8, 0, 0)
-        copy_words(("y", 0, 0), 1, "A")
-        decode(2, 9, 0, 0)
-        skip(0, 2, 1)
-        interleave(("z", 2, 3), 0, 192, "A")
-        decode(2, 9, 0, 1)
-        skip(0, 3, 1)
-        decode(2, 9, 0, 2)
-        store_y(0, 1)
-        store_y(7, 1)
-        skip_last(5, 1)
-        skip_last(1, 1)
+        store_y(2, 0)
         store_y(0, 0)
-        skip(2, 9, 1)
-        decode(2, 8, 0, 1)
-        skip(1, 4, 1)
+        bias_first(2, 1)
+        decode(0, 1, 1, 4)
+        decode(0, 3, 1, 5)
+        decode(0, 1, 1, 5)
+        decode(0, 0, 1, 4)
         skip(1, 6, 1)
-        store_y(1, 1)
-        skip_last(2, 1)
-        decode(2, 8, 0, 2)
-        decode(2, 9, 1, 0)
-        round_y(5, 0, "A")
-        quantize(("z", 2, 3))
-        quantize(("z", 2, 5))
-        skip_last(3, 1)
-        store_y(2, 1)
-        decode(2, 9, 0, 3)
-        skip(2, 8, 0)
-        quantize(("z", 2, 4))
-        store_y(3, 1)
-        round_y(4, 0, "A")
-        round_y(2, 1, "A")
-        add_bias(9, 1)
-        decode(2, 9, 1, 1)
-        decode(2, 8, 0, 3)
-        decode(2, 8, 0, 4)
-        decode(2, 8, 0, 5)
-        decode(2, 9, 1, 2)
-        decode(2, 9, 1, 3)
-        round_y(0, 1, "A")
-        add_bias(8, 0)
-        round_y(3, 1, "A")
-        round_y(1, 1, "A")
-        store_y(5, 1)
-        store_y(7, 0)
-        turn_y(("y", 1, 0), 0)
-        quantize_y(("y", 0, 0))
-        finish(8, 0)
-        store_y(8, 0)
-        turn_y(("y", 0, 1), 1)
+        decode(0, 0, 1, 5)
+        round_y(1, 0, "A")
+        bias_first(5, 1)
+        bias_first(3, 1)
+        bias_first(1, 1)
+        decode(1, 4, 1, 4)
+        decode(1, 4, 1, 5)
+        encode(("z", 2, 2), 2)
+        interleave(("z", 2, 1), 0, 256, "A")
+        bias_first(4, 1)
+        skip(1, 4, 0)
+        round_y(3, 0, "A")
+        decode(1, 7, 1, 0)
+        interleave(("z", 2, 2), 0, 256, "A")
+        skip_last(4, 0)
+        skip(1, 6, 0)
+        skip_last(6, 0)
+        decode(1, 7, 1, 1)
+        skip(1, 4, 1)
+        skip(1, 7, 1)
+        decode(1, 7, 1, 2)
+        interleave(("z", 2, 3), 0, 256, "G")
         skip_last(4, 1)
-        store_y(4, 1)
-        store_words(("y", 0, 0))
-        round_y(7, 1, "G")
-        skip_last(6, 1)
-        turn_y(("y", 0, 1), 0)
-        decode(2, 9, 0, 4)
-        copy_words(("y", 1, 0), 0, "A")
-        decode(2, 9, 0, 5)
-        finish(9, 0)
+        store_y(6, 0)
+        add_bias(7, 1)
+        bias_first(0, 1)
+        quantize(("z", 2, 1))
+        add_bias(6, 1)
+        turn_z(("z", 2, 4), 2)
+        turn_z(("z", 2, 5), 2)
+        round_y(2, 0, "G")
+        turn_y(("y", 0, 0), 1)
+        round_y(0, 0, "G")
+        encode(("z", 2, 4), 2)
+        turn_y(("y", 0, 0), 0)
+        quantize(("z", 2, 0))
+        decode(1, 6, 1, 5)
+        decode(1, 7, 1, 3)
+        decode(1, 7, 1, 4)
+        copy_words(("y", 0, 0), 0, "A")
+        finish(6, 1)
+        skip(2, 8, 1)
+        quantize(("z", 2, 3))
+        skip(0, 1, 1)
+        encode(("z", 2, 5), 2)
+        quantize(("z", 2, 2))
+        skip(1, 5, 1)
+        skip_last(5, 1)
+        decode(1, 7, 1, 5)
+        decode(2, 8, 0, 0)
+        skip(0, 0, 1)
+        decode(2, 8, 0, 1)
+        decode(2, 8, 0, 2)
+        decode(2, 8, 0, 3)
+        skip_last(0, 1)
+        finish(7, 1)
+        add_bias(8, 1)
+        skip_last(1, 1)
         decode(2, 8, 1, 0)
         decode(2, 8, 1, 1)
-        store_y(9, 0)
-        copy_words(("y", 0, 1), 0, "A")
-        round_y(4, 1, "G")
-        quantize_y(("y", 1, 0))
-        store_words(("y", 1, 0))
-        decode(2, 8, 1, 2)
-        skip(2, 8, 1)
-        store_y(6, 1)
-        round_y(8, 0, "A")
-        round_y(5, 1, "A")
-        round_y(9, 0, "A")
-        add_bias(8, 1)
-        decode(2, 9, 1, 4)
-        decode(2, 9, 1, 5)
-        finish(9, 1)
-        decode(2, 8, 1, 3)
-        decode(2, 8, 1, 4)
-        decode(2, 8, 1, 5)
-        copy_words(("y", 0, 1), 1, "A")
         round_y(6, 1, "A")
-        finish(8, 1)
-        turn_y(("y", 2, 0), 0)
-        round_y(9, 1, "V")
-        store_y(9, 1)
-        copy_words(("y", 2, 0), 0, "A")
+        interleave(("z", 2, 5), 32, 256, "G")
+        round_y(4, 1, "G")
+        skip(0, 2, 1)
+        copy_words(("y", 0, 0), 1, "A")
+        interleave(("z", 2, 4), 0, 256, "A")
+        skip(0, 3, 1)
+        skip_last(3, 1)
+        skip_last(2, 1)
+        quantize(("z", 2, 4))
+        decode(2, 8, 1, 2)
+        decode(2, 9, 1, 0)
+        skip(1, 7, 0)
+        round_y(7, 1, "A")
+        interleave(("z", 2, 5), 0, 32, "A")
+        decode(2, 8, 1, 3)
+        skip(1, 5, 0)
+        round_y(5, 1, "A")
+        skip(2, 9, 1)
+        decode(2, 9, 1, 1)
+        decode(2, 9, 1, 2)
+        decode(2, 9, 1, 3)
+        round_y(3, 1, "A")
+        round_y(0, 1, "A")
         turn_y(("y", 1, 1), 0)
-        copy_words(("y", 1, 1), 0, "A")
-        store_y(8, 1)
-        round_y(8, 1, "V")
-        quantize_y(("y", 2, 0))
-        quantize_y(("y", 0, 1))
         turn_y(("y", 1, 1), 1)
-        store_scales(0, 0)
-        store_scales(0, 1)
-        store_words(("y", 2, 0))
-        store_words(("y", 0, 1))
+        quantize(("z", 2, 5))
+        quantize_y(("y", 0, 0))
+        decode(2, 8, 1, 4)
+        add_bias(9, 1)
+        skip_last(7, 0)
+        skip_last(5, 0)
+        decode(2, 9, 1, 4)
+        skip(2, 9, 0)
+        store_y(1, 0)
+        decode(2, 8, 1, 5)
+        store_y(6, 1)
+        round_y(2, 1, "G")
+        store_y(4, 1)
+        store_y(5, 1)
+        round_y(1, 1, "A")
+        decode(2, 9, 1, 5)
+        turn_y(("y", 0, 1), 0)
         copy_words(("y", 1, 1), 1, "A")
+        round_y(4, 0, "A")
+        store_y(0, 1)
+        copy_words(("y", 1, 1), 0, "A")
+        turn_y(("y", 0, 1), 1)
+        round_y(6, 0, "G")
+        store_y(4, 0)
+        decode(2, 8, 0, 4)
+        decode(2, 8, 0, 5)
+        store_y(7, 1)
+        store_y(3, 1)
+        store_y(2, 1)
+        store_y(1, 1)
+        store_words(("y", 0, 0))
+        decode(2, 9, 0, 0)
+        finish(8, 1)
+        decode(2, 9, 0, 1)
+        decode(2, 9, 0, 2)
+        decode(2, 9, 0, 3)
+        decode(2, 9, 0, 4)
+        decode(2, 9, 0, 5)
+        copy_words(("y", 0, 1), 0, "A")
+        store_y(7, 0)
+        store_y(8, 1)
+        store_y(5, 0)
+        copy_words(("y", 0, 1), 1, "A")
+        finish(9, 1)
+        add_bias(9, 0)
+        finish(8, 0)
+        store_y(9, 1)
+        quantize_y(("y", 0, 1))
+        round_y(8, 1, "G")
         quantize_y(("y", 1, 1))
-        store_words(("y", 1, 1))
+        finish(9, 0)
+        round_y(9, 1, "A")
+        round_y(5, 0, "A")
+        round_y(7, 0, "A")
         turn_y(("y", 2, 1), 0)
+        turn_y(("y", 1, 0), 0)
+        round_y(8, 0, "V")
+        turn_y(("y", 1, 0), 1)
+        store_y(8, 0)
+        round_y(9, 0, "V")
+        store_words(("y", 0, 1))
+        store_words(("y", 1, 1))
         copy_words(("y", 2, 1), 0, "A")
+        store_y(9, 0)
+        copy_words(("y", 1, 0), 0, "A")
+        copy_words(("y", 1, 0), 1, "A")
         quantize_y(("y", 2, 1))
-        store_words(("y", 2, 1))
-        store_scales(1, 1)
         store_scales(1, 0)
+        store_words(("y", 2, 1))
+        quantize_y(("y", 1, 0))
+        turn_y(("y", 2, 0), 0)
+        copy_words(("y", 2, 0), 0, "A")
+        quantize_y(("y", 2, 0))
+        store_words(("y", 1, 0))
+        store_words(("y", 2, 0))
+        store_scales(0, 0)
+        store_scales(1, 1)
+        store_scales(0, 1)

from contextlib import ExitStack

import concourse.mybir as mybir
from concourse.masks import make_identity

M, F, C, D = 1280, 3072, 512, 1024
FLOPS = 2 * M * (F + C) * D

F32 = mybir.dt.float32
BF16 = mybir.dt.bfloat16
U32 = mybir.dt.uint32
I32 = mybir.dt.int32
U8 = mybir.dt.uint8
FP8X4 = mybir.dt.float8_e4m3fn_x4
ALU = mybir.AluOpType
ACT = mybir.ActivationFunctionType

P = 128
PACK = 4
KP = P * PACK
G = F // KP
HALF = 512
CHUNKS = [(0, 4), (4, 4), (8, 2)]
B_ROW, R_ROW = 8, 16


def tile_sae_relu_decode_skip_g1_kernel(tc, pre, b_enc, g, w_dec, b_dec, r, x, w_skip, out_0, out_1, out_2):
    nc = tc.nc
    with ExitStack() as ctx:
        keep = ctx.enter_context(tc.tile_pool(name="keep", bufs=1))
        work = ctx.enter_context(tc.tile_pool(name="work", bufs=1))
        psum = ctx.enter_context(tc.psum_pool(name="psum", bufs=1))
        ctx.enter_context(tc.manual_schedule())

        ident = keep.tile([P, P], F32, name="ident")
        ident_bf = keep.tile([P, P], BF16, name="ident_bf")
        vec_rows = keep.tile([P, KP], BF16, name="vec_rows")
        half_sign = keep.tile([P, 2, 2 * G], F32, name="half_sign")
        g_abs = keep.tile([P, 2, 2 * G], F32, name="g_abs")
        gb = keep.tile([P, 2, 2 * G], F32, name="gb")
        r_col = keep.tile([P, M // P], F32, name="r_col")
        b_all = keep.tile([P, D], BF16, name="b_all")
        y_codes = [keep.tile([P, M], U32, name="y_codes%d" % n, align_bytes=64) for n in range(2)]
        y_scales = [keep.tile([P, M], U8, name="y_scales%d" % n, align_bytes=64) for n in range(2)]

        raw, slots, grouped, codes, scales, banks, part, ybf = {}, {}, {}, {}, {}, {}, {}, {}
        free_banks = list(range(8))
        held = {}

        def take(key, shape, dtype):
            held[key] = free_banks.pop(0)
            banks[key] = psum.tile(shape, dtype, name="bank%d" % held[key])
            return banks[key]

        def release(key):
            free_banks.append(held.pop(key))

        def width(u):
            return CHUNKS[u[1]][1] * P if u[0] in "zxy" else HALF

        def move(engine, dst, src):
            if engine == "A":
                nc.scalar.copy(out=dst, in_=src)
            elif engine == "V":
                nc.vector.tensor_copy(out=dst, in_=src)
            else:
                nc.gpsimd.tensor_scalar(out=dst, in0=src, scalar1=1.0, scalar2=-0.0, op0=ALU.mult, op1=ALU.add)

        def constants_zero():
            nc.vector.memset(vec_rows[:].bitcast(U32), 0)

        def identity():
            make_identity(nc, ident[:])

        def identity_bf():
            nc.scalar.copy(out=ident_bf[:], in_=ident[:])

        def constants_load():
            for vec, row in ((g, 0), (b_enc, B_ROW)):
                rows = vec.rearrange("(c k) -> c k", k=KP)
                nc.sync.dma_start(out=vec_rows[row:row + 4, :], in_=rows[0:4])
                nc.sync.dma_start(out=vec_rows[row + 4:row + G, :], in_=rows[4:G])

        def load_half(u, h):
            if u not in raw:
                raw[u] = work.tile([P, 2, PACK, HALF // 2], BF16, name="raw", bufs=10)
            cols = slice(h * HALF // 2, (h + 1) * HALF // 2)
            nc.sync.dma_start(out=raw[u][:, h], in_=w_skip[:, cols].rearrange("(p j) d -> p j d", j=PACK))

        def constants_turn():
            bank = take("vec", [P, 2, P], F32)
            for h in range(2):
                nc.tensor.transpose(bank[:, h, :], vec_rows[:].bitcast(F32)[:, h::2], ident[:])

        def vec_cols(row):
            vals = banks["vec"][:].rearrange("p h c -> p (h c)").bitcast(BF16).rearrange("p (h v) -> p h v", h=2)
            return vals[:, :, 2 * row:2 * (row + G)]

        def sign_make():
            nc.vector.tensor_scalar(out=half_sign[:], in0=vec_cols(0), scalar1=0.0, scalar2=-0.5, op0=ALU.is_ge, op1=ALU.add)

        def constants_make():
            nc.vector.scalar_tensor_tensor(out=g_abs[:], in0=vec_cols(0), scalar=2.0, in1=half_sign[:], op0=ALU.mult, op1=ALU.mult)
            nc.vector.tensor_tensor(out=gb[:], in0=vec_cols(B_ROW), in1=g_abs[:], op=ALU.mult)
            release("vec")

        def per_k(t, k, j):
            col = 2 * k + j % 2
            return t[:, j // 2, col:col + 1]

        def r_load():
            rows = r.rearrange("(m p) o -> m (p o)", p=P)
            nc.sync.dma_start(out=vec_rows[R_ROW:R_ROW + M // P, 0:P], in_=rows)

        def r_turn():
            nc.tensor.transpose(take("r", [P, P], BF16)[:], vec_rows[:, 0:P], ident_bf[:])

        def r_copy():
            nc.scalar.copy(out=r_col[:], in_=banks["r"][:, R_ROW:R_ROW + M // P])
            release("r")

        def bias_load():
            nc.sync.dma_start(out=b_all[:], in_=b_dec.partition_broadcast(P))

        def load(u):
            kind, a, b = u
            t = work.tile([P, PACK, KP], BF16, name="raw", bufs=10)
            raw[u] = t
            if kind in "zx":
                m0, nm = CHUNKS[a]
                src = (pre if kind == "z" else x)[m0 * P:(m0 + nm) * P, b * KP:(b + 1) * KP]
                nc.sync.dma_start(out=t[:, 0:nm, :], in_=src.rearrange("(m p) k -> p m k", p=P))
            else:
                src = (w_dec if kind == "w" else w_skip)[b * KP:(b + 1) * KP, a * HALF:(a + 1) * HALF]
                nc.sync.dma_start(out=t[:], in_=src.rearrange("(p j) d -> p j d", j=PACK))

        def halves(h):
            return (0, 1) if h == 2 else (h,)

        def turn_z(u, h):
            nm = CHUNKS[u[1]][1]
            bank = take((u, h), [P, len(halves(h)), nm * P], F32)
            for i, hh in enumerate(halves(h)):
                for m in range(nm):
                    nc.tensor.transpose(bank[:, i, m * P:(m + 1) * P], raw[u][:, m, :].bitcast(F32)[:, hh::2], ident[:])

        def encode(u, h):
            w = width(u)
            if u not in slots:
                slots[u] = work.tile([P, PACK, KP], BF16, name="slots", bufs=3)
            for i, hh in enumerate(halves(h)):
                for e in range(2):
                    j = 2 * hh + e
                    nc.scalar.activation(out=slots[u][:, j, 0:w], in_=banks[u, h][:, i, :].bitcast(BF16)[:, e::2], func=ACT.Relu,
                                         bias=per_k(gb, u[2], j), scale=per_k(g_abs, u[2], j))
            release((u, h))

        def sign_w(u):
            for j in range(PACK):
                nc.vector.tensor_scalar(out=raw[u][:, j, :], in0=raw[u][:, j, :], scalar1=per_k(half_sign, u[2], j),
                                        scalar2=2.0, op0=ALU.mult, op1=ALU.mult)

        def new_grouped(u):
            if u not in grouped:
                grouped[u] = work.tile([P, KP * PACK], BF16, name="grouped", bufs=5, align_bytes=64)
            return grouped[u]

        def interleave(u, c0, c1, engine):
            if u == ("s", 0, 0):
                h = c0 // (HALF // 2)
                rows = raw[u][:, h, :, c0 - h * HALF // 2:c1 - h * HALF // 2]
            else:
                rows = slots.get(u, raw[u])[:, :, c0:c1]
            run = 1 if engine == "G" else 4
            src = rows.rearrange("p t (c i) -> p c t i", i=run)
            dst = new_grouped(u)[:, c0 * PACK:c1 * PACK].rearrange("p (c i t) -> p c t i", i=run, t=PACK)
            move(engine, dst, src)

        def quantize(u):
            w = width(u)
            name = "%s%d%d" % u
            codes[u] = keep.tile([P, w], U32, name="codes_" + name, align_bytes=64)
            scales[u] = keep.tile([P, w], U8, name="scales_" + name, align_bytes=64)
            nc.vector.quantize_mx(out=codes[u][:].bitcast(FP8X4), scales=scales[u][:], in_=grouped[u][:, 0:w * PACK])

        def turn_words(u, pair, words_of):
            bank = take((u, pair), [P, 2, 2, P], F32)
            for m in range(2):
                for h in range(2):
                    nc.tensor.transpose(bank[:, m, h, :], words_of(2 * pair + m, h), ident[:])

        def turn_x(u, pair):
            turn_words(u, pair, lambda m, h: raw[u][:, m, :].bitcast(F32)[:, h::2])

        def turn_y(u, pair):
            m0 = CHUNKS[u[1]][0]
            turn_words(u, pair, lambda m, h: ybf[m0 + m, u[2]][:].bitcast(F32)[:, h * P:(h + 1) * P])

        def copy_words(u, pair, engine):
            dst = new_grouped(u)[:].bitcast(F32)[:, pair * KP:(pair + 1) * KP].rearrange("p (m c h) -> p m c h", m=2, h=2)
            move(engine, dst, banks[u, pair][:].rearrange("p m h c -> p m c h"))
            release((u, pair))

        def mx(out, a, m, b, start, stop):
            cols = slice((m - CHUNKS[a[1]][0]) * P, (m - CHUNKS[a[1]][0] + 1) * P)
            nc.tensor.matmul_mx(out=out[:], lhsT=codes[a][:, cols].bitcast(FP8X4), lhsT_scale=scales[a][:, cols],
                                rhs=codes[b][:].bitcast(FP8X4), rhs_scale=scales[b][:], start=start, stop=stop)

        def decode(c, m, n, k):
            if k == 0:
                take(("acc", m, n), [P, HALF], F32)
            mx(banks["acc", m, n], ("z", c, k), m, ("w", n, k), k == 0, k == G - 1)

        def skip(c, m, n):
            mx(take(("skip", m, n), [P, HALF], F32), ("x", c, 0), m, ("s", n, 0), True, True)

        def new_y(m, n):
            part[m, n] = work.tile([P, HALF], F32, name="y", bufs=18)
            return part[m, n]

        def add_bias(m, n):
            nc.vector.scalar_tensor_tensor(out=new_y(m, n)[:], in0=b_all[:, n * HALF:(n + 1) * HALF], scalar=r_col[:, m:m + 1],
                                           in1=banks["skip", m, n][:], op0=ALU.mult, op1=ALU.add)
            release(("skip", m, n))

        def finish(m, n):
            y = part[m, n]
            nc.vector.scalar_tensor_tensor(out=y[:], in0=banks["acc", m, n][:], scalar=r_col[:, m:m + 1], in1=y[:],
                                           op0=ALU.mult, op1=ALU.add)
            release(("acc", m, n))

        def bias_first(m, n):
            nc.vector.tensor_tensor(out=new_y(m, n)[:], in0=banks["acc", m, n][:], in1=b_all[:, n * HALF:(n + 1) * HALF], op=ALU.add)
            release(("acc", m, n))

        def skip_last(m, n):
            y = part[m, n]
            nc.vector.scalar_tensor_tensor(out=y[:], in0=y[:], scalar=r_col[:, m:m + 1], in1=banks["skip", m, n][:],
                                           op0=ALU.mult, op1=ALU.add)
            release(("skip", m, n))

        def store_y(m, n):
            nc.sync.dma_start(out=out_0[m * P:(m + 1) * P, n * HALF:(n + 1) * HALF], in_=part[m, n][:])

        def round_y(m, n, engine):
            ybf[m, n] = work.tile([P, HALF], BF16, name="ybf", bufs=6)
            dst = ybf[m, n][:].rearrange("p (h q e) -> p h q e", h=2, e=2)
            move(engine, dst, part[m, n][:].rearrange("p (q h e) -> p h q e", h=2, e=2))

        def token_cols(u):
            return slice(CHUNKS[u[1]][0] * P, CHUNKS[u[1]][0] * P + width(u))

        def quantize_y(u):
            nc.vector.quantize_mx(out=y_codes[u[2]][:, token_cols(u)].bitcast(FP8X4), scales=y_scales[u[2]][:, token_cols(u)],
                                  in_=grouped[u][:, 0:width(u) * PACK])

        def store_words(u):
            dst = out_1[u[2]].rearrange("p m t -> p (m t)").bitcast(I32)
            nc.sync.dma_start(out=dst[:, token_cols(u)], in_=y_codes[u[2]][:, token_cols(u)].bitcast(I32))

        def store_scales(n, h):
            eng = nc.scalar if n and h else nc.sync
            for q in range(2 * h, 2 * h + 2):
                eng.dma_start(out=out_2[n, 4 * q:4 * q + 4, :].bitcast(I32),
                              in_=y_scales[n][32 * q:32 * q + 4, :].bitcast(I32))

        identity()
        constants_zero()
        load(("z", 0, 0))
        constants_load()
        load(("w", 0, 0))
        load(("z", 0, 2))
        load(("z", 0, 4))
        identity_bf()
        constants_turn()
        turn_z(("z", 0, 0), 1)
        load(("w", 0, 2))
        turn_z(("z", 0, 0), 0)
        turn_z(("z", 0, 2), 1)
        sign_make()
        constants_make()
        turn_z(("z", 0, 2), 0)
        load(("z", 0, 1))
        encode(("z", 0, 0), 1)
        load(("w", 0, 1))
        turn_z(("z", 0, 4), 0)
        load(("z", 0, 5))
        load(("z", 0, 3))
        turn_z(("z", 0, 4), 1)
        sign_w(("w", 0, 0))
        interleave(("w", 0, 0), 0, 512, "V")
        quantize(("w", 0, 0))
        encode(("z", 0, 0), 0)
        interleave(("z", 0, 0), 0, 512, "V")
        turn_z(("z", 0, 1), 0)
        encode(("z", 0, 2), 1)
        sign_w(("w", 0, 2))
        turn_z(("z", 0, 1), 1)
        quantize(("z", 0, 0))
        encode(("z", 0, 4), 0)
        encode(("z", 0, 4), 1)
        encode(("z", 0, 2), 0)
        load(("x", 0, 0))
        interleave(("w", 0, 2), 0, 512, "V")
        interleave(("z", 0, 4), 0, 512, "V")
        encode(("z", 0, 1), 0)
        encode(("z", 0, 1), 1)
        interleave(("z", 0, 2), 0, 192, "A")
        sign_w(("w", 0, 1))
        interleave(("z", 0, 2), 192, 512, "V")
        load(("w", 0, 3))
        load(("z", 1, 0))
        load(("z", 1, 2))
        load(("z", 1, 1))
        turn_z(("z", 0, 5), 1)
        turn_z(("z", 0, 3), 1)
        turn_z(("z", 0, 3), 0)
        turn_z(("z", 0, 5), 0)
        decode(0, 1, 0, 0)
        encode(("z", 0, 5), 1)
        encode(("z", 0, 5), 0)
        interleave(("w", 0, 1), 0, 512, "V")
        turn_x(("x", 0, 0), 0)
        encode(("z", 0, 3), 1)
        quantize(("z", 0, 4))
        interleave(("z", 0, 1), 0, 512, "V")
        load(("w", 0, 5))
        load(("z", 1, 3))
        sign_w(("w", 0, 3))
        quantize(("w", 0, 2))
        decode(0, 3, 0, 0)
        turn_x(("x", 0, 0), 1)
        quantize(("z", 0, 1))
        turn_z(("z", 1, 0), 1)
        turn_z(("z", 1, 0), 0)
        turn_z(("z", 1, 1), 0)
        encode(("z", 0, 3), 0)
        encode(("z", 1, 0), 1)
        load(("w", 1, 0))
        encode(("z", 1, 0), 0)
        copy_words(("x", 0, 0), 1, "A")
        r_load()
        load(("w", 0, 4))
        interleave(("z", 0, 5), 0, 512, "V")
        interleave(("z", 0, 3), 0, 512, "V")
        quantize(("w", 0, 1))
        quantize(("z", 0, 5))
        encode(("z", 1, 1), 0)
        turn_z(("z", 1, 2), 1)
        load(("x", 2, 0))
        turn_z(("z", 1, 1), 1)
        interleave(("z", 1, 0), 0, 512, "V")
        interleave(("w", 0, 3), 160, 512, "V")
        sign_w(("w", 0, 5))
        quantize(("z", 1, 0))
        decode(0, 0, 0, 0)
        encode(("z", 1, 1), 1)
        decode(0, 0, 0, 1)
        decode(0, 3, 0, 1)
        load(("z", 1, 4))
        turn_z(("z", 1, 2), 0)
        turn_z(("z", 1, 3), 1)
        decode(0, 1, 0, 1)
        interleave(("w", 0, 3), 0, 160, "A")
        encode(("z", 1, 2), 1)
        copy_words(("x", 0, 0), 0, "A")
        turn_z(("z", 1, 3), 0)
        encode(("z", 1, 3), 1)
        turn_x(("x", 2, 0), 0)
        copy_words(("x", 2, 0), 0, "A")
        turn_z(("z", 1, 4), 1)
        decode(0, 2, 0, 0)
        decode(0, 2, 0, 1)
        r_turn()
        load(("z", 1, 5))
        quantize(("z", 0, 2))
        encode(("z", 1, 2), 0)
        quantize(("w", 0, 3))
        load(("z", 2, 2))
        decode(0, 0, 0, 2)
        decode(0, 1, 0, 2)
        sign_w(("w", 0, 4))
        interleave(("z", 1, 1), 0, 512, "V")
        interleave(("w", 0, 5), 256, 512, "V")
        quantize(("z", 0, 3))
        quantize(("z", 1, 1))
        interleave(("w", 0, 4), 0, 512, "V")
        r_copy()
        encode(("z", 1, 3), 0)
        decode(0, 2, 0, 2)
        interleave(("z", 1, 2), 0, 512, "V")
        encode(("z", 1, 4), 1)
        interleave(("w", 0, 5), 0, 256, "A")
        decode(1, 5, 0, 0)
        decode(0, 3, 0, 2)
        decode(0, 0, 0, 3)
        decode(1, 5, 0, 1)
        quantize(("w", 0, 4))
        decode(0, 3, 0, 3)
        turn_z(("z", 1, 4), 0)
        load(("z", 2, 3))
        load_half(("s", 0, 0), 0)
        load(("z", 2, 1))
        turn_z(("z", 1, 5), 0)
        encode(("z", 1, 4), 0)
        load(("x", 1, 0))
        load_half(("s", 0, 0), 1)
        turn_z(("z", 1, 5), 1)
        decode(0, 2, 0, 3)
        decode(0, 3, 0, 4)
        decode(0, 1, 0, 3)
        quantize(("w", 0, 5))
        sign_w(("w", 1, 0))
        quantize(("x", 0, 0))
        bias_load()
        interleave(("w", 1, 0), 0, 512, "V")
        load(("w", 1, 3))
        turn_x(("x", 1, 0), 1)
        decode(0, 1, 0, 4)
        decode(0, 1, 0, 5)
        decode(0, 3, 0, 5)
        decode(0, 2, 0, 4)
        quantize(("x", 2, 0))
        load(("z", 2, 0))
        encode(("z", 1, 5), 0)
        encode(("z", 1, 5), 1)
        quantize(("w", 1, 0))
        quantize(("z", 1, 2))
        copy_words(("x", 1, 0), 1, "A")
        load(("s", 1, 0))
        interleave(("z", 1, 3), 0, 512, "A")
        decode(0, 2, 0, 5)
        decode(0, 0, 0, 4)
        decode(0, 0, 0, 5)
        bias_first(0, 0)
        bias_first(2, 0)
        bias_first(1, 0)
        bias_first(3, 0)
        load(("w", 1, 1))
        decode(1, 6, 0, 0)
        decode(1, 6, 0, 1)
        turn_z(("z", 2, 3), 2)
        quantize(("z", 1, 3))
        interleave(("s", 0, 0), 256, 424, "V")
        sign_w(("w", 1, 1))
        interleave(("z", 1, 4), 192, 512, "G")
        interleave(("z", 1, 5), 0, 352, "A")
        interleave(("s", 0, 0), 424, 512, "A")
        turn_z(("z", 2, 2), 2)
        turn_x(("x", 1, 0), 0)
        interleave(("z", 1, 4), 0, 192, "A")
        copy_words(("x", 1, 0), 0, "A")
        interleave(("s", 0, 0), 168, 256, "A")
        load(("w", 1, 2))
        sign_w(("w", 1, 3))
        load(("w", 1, 5))
        decode(1, 4, 0, 0)
        decode(1, 6, 0, 2)
        decode(1, 7, 0, 0)
        decode(1, 5, 0, 2)
        decode(1, 7, 0, 1)
        decode(1, 7, 0, 2)
        decode(1, 7, 0, 3)
        interleave(("z", 1, 5), 352, 512, "V")
        quantize(("z", 1, 4))
        interleave(("s", 0, 0), 0, 168, "V")
        interleave(("w", 1, 1), 0, 512, "A")
        quantize(("z", 1, 5))
        decode(1, 5, 0, 3)
        decode(1, 4, 0, 1)
        decode(1, 4, 0, 2)
        decode(1, 4, 0, 3)
        turn_z(("z", 2, 0), 2)
        turn_z(("z", 2, 1), 2)
        quantize(("s", 0, 0))
        sign_w(("w", 1, 2))
        quantize(("w", 1, 1))
        decode(1, 5, 0, 4)
        encode(("z", 2, 1), 2)
        decode(1, 7, 0, 4)
        decode(1, 6, 0, 3)
        decode(1, 5, 0, 5)
        decode(1, 6, 0, 4)
        decode(1, 6, 0, 5)
        bias_first(6, 0)
        decode(1, 7, 0, 5)
        decode(1, 4, 0, 4)
        decode(1, 4, 0, 5)
        bias_first(4, 0)
        encode(("z", 2, 3), 2)
        decode(1, 6, 1, 0)
        decode(1, 6, 1, 1)
        bias_first(5, 0)
        bias_first(7, 0)
        decode(0, 3, 1, 0)
        decode(0, 3, 1, 1)
        encode(("z", 2, 0), 2)
        skip(0, 1, 0)
        decode(1, 5, 1, 0)
        skip(0, 0, 0)
        decode(1, 5, 1, 1)
        skip_last(1, 0)
        interleave(("w", 1, 2), 128, 512, "G")
        skip(0, 2, 0)
        decode(1, 4, 1, 0)
        load(("w", 1, 4))
        load(("z", 2, 4))
        skip_last(0, 0)
        load(("z", 2, 5))
        skip_last(2, 0)
        skip(0, 3, 0)
        decode(1, 4, 1, 1)
        decode(0, 0, 1, 0)
        decode(0, 0, 1, 1)
        decode(0, 2, 1, 0)
        interleave(("w", 1, 2), 0, 128, "A")
        interleave(("w", 1, 3), 0, 416, "A")
        quantize(("w", 1, 2))
        decode(0, 2, 1, 1)
        decode(0, 3, 1, 2)
        sign_w(("w", 1, 4))
        decode(0, 2, 1, 2)
        decode(1, 4, 1, 2)
        skip_last(3, 0)
        interleave(("w", 1, 3), 416, 512, "G")
        quantize(("w", 1, 3))
        decode(0, 0, 1, 2)
        interleave(("w", 1, 4), 0, 512, "A")
        sign_w(("w", 1, 5))
        skip(2, 8, 0)
        decode(1, 5, 1, 2)
        decode(1, 6, 1, 2)
        decode(1, 5, 1, 3)
        add_bias(8, 0)
        decode(0, 0, 1, 3)
        decode(0, 3, 1, 3)
        interleave(("w", 1, 5), 0, 288, "A")
        interleave(("w", 1, 5), 288, 512, "V")
        interleave(("s", 1, 0), 0, 224, "A")
        interleave(("z", 2, 0), 0, 256, "A")
        quantize(("w", 1, 4))
        decode(0, 2, 1, 3)
        decode(0, 1, 1, 0)
        decode(0, 1, 1, 1)
        interleave(("s", 1, 0), 224, 512, "V")
        decode(0, 1, 1, 2)
        decode(1, 4, 1, 3)
        decode(0, 1, 1, 3)
        decode(1, 5, 1, 4)
        quantize(("w", 1, 5))
        quantize(("x", 1, 0))
        decode(0, 2, 1, 4)
        quantize(("s", 1, 0))
        decode(0, 3, 1, 4)
        decode(1, 6, 1, 3)
        decode(1, 6, 1, 4)
        decode(0, 2, 1, 5)
        decode(1, 5, 1, 5)
        store_y(3, 0)
        store_y(2, 0)
        store_y(0, 0)
        bias_first(2, 1)
        decode(0, 1, 1, 4)
        decode(0, 3, 1, 5)
        decode(0, 1, 1, 5)
        decode(0, 0, 1, 4)
        skip(1, 6, 1)
        decode(0, 0, 1, 5)
        round_y(1, 0, "A")
        bias_first(5, 1)
        bias_first(3, 1)
        bias_first(1, 1)
        decode(1, 4, 1, 4)
        decode(1, 4, 1, 5)
        encode(("z", 2, 2), 2)
        interleave(("z", 2, 1), 0, 256, "A")
        bias_first(4, 1)
        skip(1, 4, 0)
        round_y(3, 0, "A")
        decode(1, 7, 1, 0)
        interleave(("z", 2, 2), 0, 256, "A")
        skip_last(4, 0)
        skip(1, 6, 0)
        skip_last(6, 0)
        decode(1, 7, 1, 1)
        skip(1, 4, 1)
        skip(1, 7, 1)
        decode(1, 7, 1, 2)
        interleave(("z", 2, 3), 0, 256, "G")
        skip_last(4, 1)
        store_y(6, 0)
        add_bias(7, 1)
        bias_first(0, 1)
        quantize(("z", 2, 1))
        add_bias(6, 1)
        turn_z(("z", 2, 4), 2)
        turn_z(("z", 2, 5), 2)
        round_y(2, 0, "G")
        turn_y(("y", 0, 0), 1)
        round_y(0, 0, "G")
        encode(("z", 2, 4), 2)
        turn_y(("y", 0, 0), 0)
        quantize(("z", 2, 0))
        decode(1, 6, 1, 5)
        decode(1, 7, 1, 3)
        decode(1, 7, 1, 4)
        copy_words(("y", 0, 0), 0, "A")
        finish(6, 1)
        skip(2, 8, 1)
        quantize(("z", 2, 3))
        skip(0, 1, 1)
        encode(("z", 2, 5), 2)
        quantize(("z", 2, 2))
        skip(1, 5, 1)
        skip_last(5, 1)
        decode(1, 7, 1, 5)
        decode(2, 8, 0, 0)
        skip(0, 0, 1)
        decode(2, 8, 0, 1)
        decode(2, 8, 0, 2)
        decode(2, 8, 0, 3)
        skip_last(0, 1)
        finish(7, 1)
        add_bias(8, 1)
        skip_last(1, 1)
        decode(2, 8, 1, 0)
        decode(2, 8, 1, 1)
        round_y(6, 1, "A")
        interleave(("z", 2, 5), 32, 256, "G")
        round_y(4, 1, "G")
        skip(0, 2, 1)
        copy_words(("y", 0, 0), 1, "A")
        interleave(("z", 2, 4), 0, 256, "A")
        skip(0, 3, 1)
        skip_last(3, 1)
        skip_last(2, 1)
        quantize(("z", 2, 4))
        decode(2, 8, 1, 2)
        decode(2, 9, 1, 0)
        skip(1, 7, 0)
        round_y(7, 1, "A")
        interleave(("z", 2, 5), 0, 32, "A")
        decode(2, 8, 1, 3)
        skip(1, 5, 0)
        round_y(5, 1, "A")
        skip(2, 9, 1)
        decode(2, 9, 1, 1)
        decode(2, 9, 1, 2)
        decode(2, 9, 1, 3)
        round_y(3, 1, "A")
        round_y(0, 1, "A")
        turn_y(("y", 1, 1), 0)
        turn_y(("y", 1, 1), 1)
        quantize(("z", 2, 5))
        quantize_y(("y", 0, 0))
        decode(2, 8, 1, 4)
        add_bias(9, 1)
        skip_last(7, 0)
        skip_last(5, 0)
        decode(2, 9, 1, 4)
        skip(2, 9, 0)
        store_y(1, 0)
        decode(2, 8, 1, 5)
        store_y(6, 1)
        round_y(2, 1, "G")
        store_y(4, 1)
        store_y(5, 1)
        round_y(1, 1, "A")
        decode(2, 9, 1, 5)
        turn_y(("y", 0, 1), 0)
        copy_words(("y", 1, 1), 1, "A")
        round_y(4, 0, "A")
        store_y(0, 1)
        copy_words(("y", 1, 1), 0, "A")
        turn_y(("y", 0, 1), 1)
        round_y(6, 0, "G")
        store_y(4, 0)
        decode(2, 8, 0, 4)
        decode(2, 8, 0, 5)
        store_y(7, 1)
        store_y(3, 1)
        store_y(2, 1)
        store_y(1, 1)
        store_words(("y", 0, 0))
        decode(2, 9, 0, 0)
        finish(8, 1)
        decode(2, 9, 0, 1)
        decode(2, 9, 0, 2)
        decode(2, 9, 0, 3)
        decode(2, 9, 0, 4)
        decode(2, 9, 0, 5)
        copy_words(("y", 0, 1), 0, "A")
        store_y(7, 0)
        store_y(8, 1)
        store_y(5, 0)
        copy_words(("y", 0, 1), 1, "A")
        finish(9, 1)
        add_bias(9, 0)
        finish(8, 0)
        store_y(9, 1)
        quantize_y(("y", 0, 1))
        round_y(8, 1, "G")
        quantize_y(("y", 1, 1))
        finish(9, 0)
        round_y(9, 1, "A")
        round_y(5, 0, "A")
        round_y(7, 0, "A")
        turn_y(("y", 2, 1), 0)
        turn_y(("y", 1, 0), 0)
        round_y(8, 0, "V")
        turn_y(("y", 1, 0), 1)
        store_y(8, 0)
        round_y(9, 0, "V")
        store_words(("y", 0, 1))
        store_words(("y", 1, 1))
        copy_words(("y", 2, 1), 0, "A")
        store_y(9, 0)
        copy_words(("y", 1, 0), 0, "A")
        copy_words(("y", 1, 0), 1, "A")
        quantize_y(("y", 2, 1))
        store_scales(1, 0)
        store_words(("y", 2, 1))
        quantize_y(("y", 1, 0))
        turn_y(("y", 2, 0), 0)
        copy_words(("y", 2, 0), 0, "A")
        quantize_y(("y", 2, 0))
        store_words(("y", 1, 0))
        store_words(("y", 2, 0))
        store_scales(0, 0)
        store_scales(1, 1)
        store_scales(0, 1)
